import numpy as np
import ml_dtypes


def mxq(x, axis, fmt="e4m3"):
    dtype, down = {"e4m3": (ml_dtypes.float8_e4m3fn, 7), "e5m2": (ml_dtypes.float8_e5m2, 14)}[fmt]
    v = np.moveaxis(np.asarray(x, np.float32).astype(ml_dtypes.bfloat16).astype(np.float64), axis, -1)
    blocks = v.reshape(v.shape[:-1] + (-1, 32))
    amax = np.abs(blocks).max(-1, keepdims=True)
    byte = np.maximum(np.where(amax > 0, np.frexp(amax)[1] - 1 + 127, 0) - down, 1)
    scale = np.exp2(byte - 127.0)
    codes = (blocks / scale).astype(np.float32).astype(dtype).astype(np.float64)
    return np.moveaxis((codes * scale).reshape(v.shape), -1, axis)


WIDE = False


def mx_kscale(k):
    if not WIDE:
        return np.ones(k)
    levels = np.array([10, -10, 5, -5, 0])
    if k % 512:
        return np.exp2(np.random.permutation(np.resize(levels, k // 32))).repeat(32)
    a = np.empty((k // 512, 16))
    for p in range(k // 512):
        a[p, :8] = np.random.permutation(np.resize(levels, 8))
        for g in range(8):
            far = levels[np.abs(levels - a[p, g]) >= 10]
            a[p, g + 8] = far[np.random.randint(len(far))]
    return np.exp2(a.ravel()).repeat(32)


def f64(x):
    return np.asarray(x).astype(np.float64)


def striped(idx):
    return np.tile(np.asarray(idx).reshape(-1, 16).T, (8, 1)).astype(np.uint16)


def unstriped(offs):
    return offs[:16].T.reshape(-1).astype(np.int64)


E2M1 = np.array([0.0, 0.5, 1.0, 1.5, 2.0, 3.0, 4.0, 6.0, -0.0, -0.5, -1.0, -1.5, -2.0, -3.0, -4.0, -6.0])


def pack_weight(w, fmt):
    k, n = w.shape
    w = f64(np.asarray(w, np.float32).astype(ml_dtypes.bfloat16)).reshape(k // 32, 32, n)
    amax = np.abs(w).max(1)
    if fmt == "e4m3":
        byte = np.frexp(amax)[1] - 1 + 127 - 7
    else:
        mant, ex = np.frexp(amax / 6.0)
        byte = np.where(mant > 0.5, ex, ex - 1) + 127
    byte = np.clip(np.where(amax > 0, byte, 1), 1, 254)
    scaled = (w * np.exp2(127.0 - byte)[:, None, :]).reshape(k, n).astype(np.float32)
    by_word = np.ascontiguousarray(scaled.reshape(k // 512, 128, 4, n).transpose(0, 1, 3, 2))
    if fmt == "e4m3":
        words = by_word.astype(ml_dtypes.float8_e4m3fn).view(np.uint8)
    else:
        c = by_word.astype(ml_dtypes.float4_e2m1fn).view(np.uint8) & 0xF
        words = (c[..., 0::2] | (c[..., 1::2] << 4)).reshape(k // 512, 128, 2 * n)
    return np.ascontiguousarray(words), np.ascontiguousarray(byte.astype(np.uint8).reshape(k // 512, 16, n))


def unpack_weight(words, scales, fmt):
    g, _, n = scales.shape
    words = np.ascontiguousarray(words).reshape(g, 128, n, -1)
    if fmt == "e4m3":
        vals = words.view(ml_dtypes.float8_e4m3fn).astype(np.float64)
    else:
        nib = np.empty((g, 128, n, 4), np.uint8)
        nib[..., 0::2] = words & 0xF
        nib[..., 1::2] = words >> 4
        vals = E2M1[nib]
    vals = vals * np.repeat(np.exp2(scales.astype(np.float64) - 127.0), 8, axis=1)[..., None]
    return vals.transpose(0, 1, 3, 2).reshape(g * 512, n)


K, D, T, I, Q = 512, 512, 2048, 512, 128


def setup_inputs():
    n = np.random.standard_normal
    idx = np.random.permutation(T)[:I]
    fk = mx_kscale(K)
    fd = mx_kscale(D)
    keysp = pack_weight(n((K, T)) / fk[:, None], "e4m3")
    return {
        "query": (n((K, Q)) * 1.0 / np.sqrt(K) / fk[:, None]).astype(np.float32),
        "hq": ((np.prod([1.0 - 2.0 * (((np.arange(K)[:, None] & np.arange(D)) >> b) & 1) for b in range(9)], axis=0) / np.sqrt(K)) * fk[:, None] * fd).astype(np.float32),
        "hk": ((np.prod([1.0 - 2.0 * (((np.arange(K)[:, None] & np.arange(D)) >> b) & 1) for b in range(9)], axis=0) / np.sqrt(K)) * fk[:, None] / fd).astype(np.float32),
        "keys_words": keysp[0],
        "keys_scales": keysp[1],
        "offs": striped(idx),
    }


def reference(query, hq, hk, keys_words, keys_scales, offs):
    idx = unstriped(offs)
    keysu = unpack_weight(keys_words, keys_scales, "e4m3")
    hqq = mxq(f64(hq), 0, "e4m3")
    queryq = mxq(f64(query), 0, "e4m3")
    qr = hqq.T @ queryq
    hkq = mxq(f64(hk), 0, "e4m3")
    keysidxg = keysu[:, idx]
    kr = hkq.T @ keysidxg
    qrq = mxq(qr, 0, "e4m3")
    krq = mxq(kr, 0, "e4m3")
    a = qrq.T @ krq
    p = np.exp(a - np.max(a, axis=1, keepdims=True))
    y = p / np.sum(p, axis=1, keepdims=True) * 512.0
    return y

@@ -1,0 +1,180 @@
+from contextlib import ExitStack
+
+import concourse.mybir as mybir
+
+K, D, T, I, Q = 512, 512, 2048, 512, 128
+FLOPS = 2 * K * D * Q + 2 * K * D * I + 2 * D * Q * I
+
+F32 = mybir.dt.float32
+BF16 = mybir.dt.bfloat16
+I32 = mybir.dt.int32
+U32 = mybir.dt.uint32
+U16 = mybir.dt.uint16
+U8 = mybir.dt.uint8
+FP8X4 = mybir.dt.float8_e4m3fn_x4
+ALU = mybir.AluOpType
+ACT = mybir.ActivationFunctionType
+AX = mybir.AxisListType
+
+P = 128
+PACK = 4
+HK_PIECES = [(0, 256), (256, 512)]
+HQ_PIECES = [(0, 256), (256, 384), (384, 512)]
+
+
+def tile_attend_rotatedscores_kernel(tc, query, hq, hk, keys_words, keys_scales, offs, out):
+    nc = tc.nc
+    with ExitStack() as ctx:
+        sb = ctx.enter_context(tc.tile_pool(name="sb", bufs=1))
+        ps = ctx.enter_context(tc.psum_pool(name="ps", bufs=1))
+
+        def tile(shape, dtype, name):
+            return sb.tile(shape, dtype, name=name, align_bytes=64)
+
+        offsets = sb.tile([P, I // 16], U16, name="offsets")
+        pool_scales = tile([P, T], U8, "pool_scales")
+        pool_words = tile([P, T], I32, "pool_words")
+        nc.vector.memset(pool_scales[:].bitcast(I32), 0)
+        nc.sync.dma_start(offsets[:], offs)
+        warm_in = tile([P, 8], F32, "warm_in")
+        warm_out = tile([P, 8], F32, "warm_out")
+        nc.vector.memset(warm_in[:], 0.0)
+        nc.scalar.activation(warm_out[:], warm_in[:], ACT.Exp)
+
+        def load_piece(src, piece, name):
+            lo, hi = piece
+            raw = tile([P, PACK, hi - lo], F32, "%s_raw%d" % (name, lo))
+            nc.sync.dma_start(out=raw[:], in_=src.rearrange("(p t) d -> p t d", t=PACK)[:, :, lo:hi])
+            return raw
+
+        hk_raw = [load_piece(hk, piece, "hk") for piece in HK_PIECES]
+        for quad in range(4):
+            nc.sync.dma_start(
+                out=pool_scales[32 * quad : 32 * quad + 4, :].bitcast(I32),
+                in_=keys_scales[0, 4 * quad : 4 * quad + 4, :].bitcast(I32),
+            )
+        nc.sync.dma_start(
+            out=pool_words[:],
+            in_=keys_words[0].rearrange("p n t -> p (n t)").bitcast(I32),
+        )
+        query_raw = tile([P, PACK, Q], F32, "query_raw")
+        nc.sync.dma_start(out=query_raw[:], in_=query.rearrange("(p t) q -> p t q", t=PACK))
+        hq_raw = [load_piece(hq, piece, "hq") for piece in HQ_PIECES]
+
+        def deal(copy, raw, dealt):
+            copy(
+                out=dealt.rearrange("p j (u i t) -> p u j t i", i=4, t=PACK),
+                in_=raw.rearrange("p t (u j i) -> p u j t i", j=PACK, i=4),
+            )
+
+        hk_dealt = tile([P, PACK, D], BF16, "hk_dealt")
+        deal(nc.vector.tensor_copy, hk_raw[0][:], hk_dealt[:, :, HK_PIECES[0][0] : HK_PIECES[0][1]])
+        deal(nc.scalar.copy, hk_raw[1][:], hk_dealt[:, :, HK_PIECES[1][0] : HK_PIECES[1][1]])
+
+        key_scales = tile([P, I], U8, "key_scales")
+        nc.vector.tensor_copy(key_scales[:], pool_scales[:].indirect(offsets[:]))
+
+        hk_codes = tile([P, D], U32, "hk_codes")
+        hk_scales = tile([P, D], U8, "hk_scales")
+        nc.vector.quantize_mx(
+            out=hk_codes[:].bitcast(FP8X4), scales=hk_scales[:], in_=hk_dealt[:].rearrange("p j x -> p (j x)")
+        )
+
+        key_words = []
+        for h in range(2):
+            gathered = tile([P, I // 2], U32, "key_words%d" % h)
+            nc.vector.tensor_copy(
+                gathered[:], pool_words[:].bitcast(U32).indirect(offsets[:, 16 * h : 16 * (h + 1)])
+            )
+            key_words.append(gathered)
+
+        query_bf = tile([P, Q, PACK], BF16, "query_bf")
+        nc.scalar.copy(
+            out=query_bf[:].rearrange("p (c i) t -> p c t i", i=4),
+            in_=query_raw[:].rearrange("p t (c i) -> p c t i", i=4),
+        )
+
+        kr_bf = tile([P, I, PACK], BF16, "kr_bf")
+        for b in range(4):
+            bank = ps.tile([P, PACK, P], F32, name="kr_bank%d" % b)
+            cols = slice((b % 2) * P, (b % 2 + 1) * P)
+            for j in range(PACK):
+                nc.tensor.matmul_mx(
+                    out=bank[:, j, :],
+                    lhsT=hk_codes[:, j * P : (j + 1) * P].bitcast(FP8X4),
+                    lhsT_scale=hk_scales[:, j * P : (j + 1) * P],
+                    rhs=key_words[b // 2][:, cols].bitcast(FP8X4),
+                    rhs_scale=key_scales[:, b * P : (b + 1) * P],
+                    start=True,
+                    stop=True,
+                )
+            nc.scalar.copy(out=kr_bf[:, b * P : (b + 1) * P, :], in_=bank[:].rearrange("p j n -> p n j"))
+
+        query_codes = tile([P, Q], U32, "query_codes")
+        query_scales = tile([P, Q], U8, "query_scales")
+        nc.vector.quantize_mx(
+            out=query_codes[:].bitcast(FP8X4),
+            scales=query_scales[:],
+            in_=query_bf[:].rearrange("p q t -> p (q t)"),
+        )
+        hq_codes = [tile([P, P], U32, "hq_codes%d" % j) for j in range(PACK)]
+        hq_scales = [tile([P, P], U8, "hq_scales%d" % j) for j in range(PACK)]
+        for half in range(2):
+            dealt = tile([P, PACK, D // 2], BF16, "hq_dealt%d" % half)
+            base = half * (D // 2)
+            for raw, (lo, hi) in zip(hq_raw, HQ_PIECES):
+                if base <= lo < base + D // 2:
+                    deal(nc.vector.tensor_copy, raw[:], dealt[:, :, lo - base : hi - base])
+            cols = slice(half * (P // 2), (half + 1) * (P // 2))
+            for j in range(PACK):
+                nc.vector.quantize_mx(
+                    out=hq_codes[j][:, cols].bitcast(FP8X4), scales=hq_scales[j][:, cols], in_=dealt[:, j, :]
+                )
+
+        qr_bank = ps.tile([P, PACK, Q], F32, name="qr_bank")
+        for j in range(PACK):
+            nc.tensor.matmul_mx(
+                out=qr_bank[:, j, :],
+                lhsT=hq_codes[j][:].bitcast(FP8X4),
+                lhsT_scale=hq_scales[j][:],
+                rhs=query_codes[:].bitcast(FP8X4),
+                rhs_scale=query_scales[:],
+                start=True,
+                stop=True,
+            )
+        qr_bf = tile([P, Q, PACK], BF16, "qr_bf")
+        nc.scalar.copy(out=qr_bf[:], in_=qr_bank[:].rearrange("p j n -> p n j"))
+
+        kr_codes = tile([P, I], U32, "kr_codes")
+        kr_scales = tile([P, I], U8, "kr_scales")
+        nc.vector.quantize_mx(
+            out=kr_codes[:].bitcast(FP8X4), scales=kr_scales[:], in_=kr_bf[:].rearrange("p n j -> p (n j)")
+        )
+        qr_codes = tile([P, Q], U32, "qr_codes")
+        qr_scales = tile([P, Q], U8, "qr_scales")
+        nc.vector.quantize_mx(
+            out=qr_codes[:].bitcast(FP8X4),
+            scales=qr_scales[:],
+            in_=qr_bf[:].rearrange("p q j -> p (q j)"),
+        )
+
+        scores = ps.tile([P, I], F32, name="scores")
+        nc.tensor.matmul_mx(
+            out=scores[:],
+            lhsT=qr_codes[:].bitcast(FP8X4),
+            lhsT_scale=qr_scales[:],
+            rhs=kr_codes[:].bitcast(FP8X4),
+            rhs_scale=kr_scales[:],
+            start=True,
+            stop=True,
+        )
+        neg_max = tile([P, 1], F32, "neg_max")
+        nc.vector.tensor_reduce(neg_max[:], scores[:], AX.X, ALU.max, negate=True)
+        weights = tile([P, I], F32, "weights")
+        row_sum = tile([P, 1], F32, "row_sum")
+        nc.scalar.activation(weights[:], scores[:], ACT.Exp, bias=neg_max[:], accum_out=row_sum[:])
+        inv_sum = tile([P, 1], F32, "inv_sum")
+        nc.vector.reciprocal(inv_sum[:], row_sum[:])
+        result = tile([P, I], F32, "result")
+        nc.vector.tensor_scalar(result[:], weights[:], inv_sum[:], 512.0, ALU.mult, ALU.mult)
+        nc.sync.dma_start(out=out, in_=result[:])

@@ -28,38 +28,45 @@ def tile_attend_rotatedscores_kernel(tc, query, hq, hk, keys_words, keys_scales,
         sb = ctx.enter_context(tc.tile_pool(name="sb", bufs=1))
         ps = ctx.enter_context(tc.psum_pool(name="ps", bufs=1))
 
-        def tile(shape, dtype, name):
-            return sb.tile(shape, dtype, name=name, align_bytes=64)
+        def tile(shape, dtype, name, tag=None):
+            return sb.tile(shape, dtype, name=name, tag=tag or name, align_bytes=64)
 
         offsets = sb.tile([P, I // 16], U16, name="offsets")
         pool_scales = tile([P, T], U8, "pool_scales")
         pool_words = tile([P, T], I32, "pool_words")
         nc.vector.memset(pool_scales[:].bitcast(I32), 0)
-        nc.sync.dma_start(offsets[:], offs)
-        warm_in = tile([P, 8], F32, "warm_in")
-        warm_out = tile([P, 8], F32, "warm_out")
-        nc.vector.memset(warm_in[:], 0.0)
-        nc.scalar.activation(warm_out[:], warm_in[:], ACT.Exp)
-
-        def load_piece(src, piece, name):
-            lo, hi = piece
-            raw = tile([P, PACK, hi - lo], F32, "%s_raw%d" % (name, lo))
-            nc.sync.dma_start(out=raw[:], in_=src.rearrange("(p t) d -> p t d", t=PACK)[:, :, lo:hi])
-            return raw
-
-        hk_raw = [load_piece(hk, piece, "hk") for piece in HK_PIECES]
+        scale_rows = tile([P, T // 4], I32, "scale_rows")
         for quad in range(4):
             nc.sync.dma_start(
-                out=pool_scales[32 * quad : 32 * quad + 4, :].bitcast(I32),
+                out=scale_rows[32 * quad : 32 * quad + 4, :],
                 in_=keys_scales[0, 4 * quad : 4 * quad + 4, :].bitcast(I32),
             )
+        nc.sync.dma_start(offsets[:], offs)
+        for quad in range(4):
+            rows = slice(32 * quad, 32 * quad + 4)
+            nc.vector.tensor_copy(pool_scales[:].bitcast(I32)[rows, :], scale_rows[rows, :])
+        key_scales = tile([P, I], U8, "key_scales")
+        nc.vector.tensor_copy(key_scales[:], pool_scales[:].indirect(offsets[:]))
+
+        def load_piece(queue, src, piece, name):
+            lo, hi = piece
+            raw = tile([P, PACK, hi - lo], F32, "%s_raw%d" % (name, lo))
+            queue.dma_start(out=raw[:], in_=src.rearrange("(p t) d -> p t d", t=PACK)[:, :, lo:hi])
+            return raw
+
+        hk_raw = [load_piece(queue, hk, piece, "hk") for queue, piece in zip((nc.scalar, nc.sync), HK_PIECES)]
         nc.sync.dma_start(
             out=pool_words[:],
             in_=keys_words[0].rearrange("p n t -> p (n t)").bitcast(I32),
         )
         query_raw = tile([P, PACK, Q], F32, "query_raw")
         nc.sync.dma_start(out=query_raw[:], in_=query.rearrange("(p t) q -> p t q", t=PACK))
-        hq_raw = [load_piece(hq, piece, "hq") for piece in HQ_PIECES]
+        hq_raw = [load_piece(nc.sync, hq, piece, "hq") for piece in HQ_PIECES]
+
+        warm_in = tile([P, 8], F32, "warm_in")
+        warm_out = tile([P, 8], F32, "warm_out")
+        nc.vector.memset(warm_in[:], 0.0)
+        nc.scalar.activation(warm_out[:], warm_in[:], ACT.Exp)
 
         def deal(copy, raw, dealt):
             copy(
@@ -68,11 +75,9 @@ def tile_attend_rotatedscores_kernel(tc, query, hq, hk, keys_words, keys_scales,
             )
 
         hk_dealt = tile([P, PACK, D], BF16, "hk_dealt")
-        deal(nc.vector.tensor_copy, hk_raw[0][:], hk_dealt[:, :, HK_PIECES[0][0] : HK_PIECES[0][1]])
-        deal(nc.scalar.copy, hk_raw[1][:], hk_dealt[:, :, HK_PIECES[1][0] : HK_PIECES[1][1]])
+        deal(nc.scalar.copy, hk_raw[0][:], hk_dealt[:, :, HK_PIECES[0][0] : HK_PIECES[0][1]])
+        deal(nc.vector.tensor_copy, hk_raw[1][:], hk_dealt[:, :, HK_PIECES[1][0] : HK_PIECES[1][1]])
 
-        key_scales = tile([P, I], U8, "key_scales")
-        nc.vector.tensor_copy(key_scales[:], pool_scales[:].indirect(offsets[:]))
 
         hk_codes = tile([P, D], U32, "hk_codes")
         hk_scales = tile([P, D], U8, "hk_scales")
@@ -145,7 +150,7 @@ def tile_attend_rotatedscores_kernel(tc, query, hq, hk, keys_words, keys_scales,
         qr_bf = tile([P, Q, PACK], BF16, "qr_bf")
         nc.scalar.copy(out=qr_bf[:], in_=qr_bank[:].rearrange("p j n -> p n j"))
 
-        kr_codes = tile([P, I], U32, "kr_codes")
+        kr_codes = tile([P, I], U32, "kr_codes", tag="hq_dealt1")
         kr_scales = tile([P, I], U8, "kr_scales")
         nc.vector.quantize_mx(
             out=kr_codes[:].bitcast(FP8X4), scales=kr_scales[:], in_=kr_bf[:].rearrange("p n j -> p (n j)")
@@ -175,6 +180,8 @@ def tile_attend_rotatedscores_kernel(tc, query, hq, hk, keys_words, keys_scales,
         nc.scalar.activation(weights[:], scores[:], ACT.Exp, bias=neg_max[:], accum_out=row_sum[:])
         inv_sum = tile([P, 1], F32, "inv_sum")
         nc.vector.reciprocal(inv_sum[:], row_sum[:])
-        result = tile([P, I], F32, "result")
-        nc.vector.tensor_scalar(result[:], weights[:], inv_sum[:], 512.0, ALU.mult, ALU.mult)
-        nc.sync.dma_start(out=out, in_=result[:])
+        for half, queue in enumerate((nc.scalar, nc.sync)):
+            cols = slice(half * (I // 2), (half + 1) * (I // 2))
+            result = tile([P, I // 2], F32, "result%d" % half)
+            nc.vector.tensor_scalar(result[:], weights[:, cols], inv_sum[:], 512.0, ALU.mult, ALU.mult)
+            queue.dma_start(out=out[:, cols], in_=result[:])

@@ -18,8 +18,7 @@ AX = mybir.AxisListType
 
 P = 128
 PACK = 4
-HK_PIECES = [(0, 256), (256, 512)]
-HQ_PIECES = [(0, 256), (256, 384), (384, 512)]
+HK_SCALAR_COLS = 384
 
 
 def tile_attend_rotatedscores_kernel(tc, query, hq, hk, keys_words, keys_scales, offs, out):
@@ -34,39 +33,45 @@ def tile_attend_rotatedscores_kernel(tc, query, hq, hk, keys_words, keys_scales,
         offsets = sb.tile([P, I // 16], U16, name="offsets")
         pool_scales = tile([P, T], U8, "pool_scales")
         pool_words = tile([P, T], I32, "pool_words")
-        nc.vector.memset(pool_scales[:].bitcast(I32), 0)
         scale_rows = tile([P, T // 4], I32, "scale_rows")
-        for quad in range(4):
-            nc.sync.dma_start(
+        hk_raw = tile([P, PACK, D], F32, "hk_raw")
+        hq_raw = [tile([P, PACK, D // 2], F32, "hq_raw%d" % half) for half in range(2)]
+        query_raw = tile([P, PACK, Q], F32, "query_raw")
+        hk_rows = hk.rearrange("(p t) d -> p t d", t=PACK)
+        hq_rows = hq.rearrange("(p t) d -> p t d", t=PACK)
+
+        def load_scales(queue, quad):
+            queue.dma_start(
                 out=scale_rows[32 * quad : 32 * quad + 4, :],
                 in_=keys_scales[0, 4 * quad : 4 * quad + 4, :].bitcast(I32),
             )
+
+        def load_hq(half):
+            nc.sync.dma_start(out=hq_raw[half][:], in_=hq_rows[:, :, half * (D // 2) : (half + 1) * (D // 2)])
+
+        def load_words():
+            nc.sync.dma_start(out=pool_words[:], in_=keys_words[0].rearrange("p n t -> p (n t)").bitcast(I32))
+
+        nc.scalar.dma_start(out=hk_raw[:, 0:2, :], in_=hk_rows[:, 0:2, :])
+        for quad in (0, 2, 1, 3):
+            load_scales(nc.sync, quad)
         nc.sync.dma_start(offsets[:], offs)
-        for quad in range(4):
+        nc.sync.dma_start(out=hk_raw[:, 2:4, :], in_=hk_rows[:, 2:4, :])
+        load_hq(0)
+        load_words()
+        load_hq(1)
+        nc.sync.dma_start(out=query_raw[:], in_=query.rearrange("(p t) q -> p t q", t=PACK))
+
+        warm_in = tile([P, 8], F32, "warm_in")
+        warm_out = tile([P, 8], F32, "warm_out")
+        nc.gpsimd.memset(warm_in[:], 0.0)
+        nc.scalar.activation(warm_out[:], warm_in[:], ACT.Exp)
+        nc.vector.memset(pool_scales[:].bitcast(I32), 0)
+        for quad in (0, 2, 1, 3):
             rows = slice(32 * quad, 32 * quad + 4)
             nc.vector.tensor_copy(pool_scales[:].bitcast(I32)[rows, :], scale_rows[rows, :])
         key_scales = tile([P, I], U8, "key_scales")
         nc.vector.tensor_copy(key_scales[:], pool_scales[:].indirect(offsets[:]))
-
-        def load_piece(queue, src, piece, name):
-            lo, hi = piece
-            raw = tile([P, PACK, hi - lo], F32, "%s_raw%d" % (name, lo))
-            queue.dma_start(out=raw[:], in_=src.rearrange("(p t) d -> p t d", t=PACK)[:, :, lo:hi])
-            return raw
-
-        hk_raw = [load_piece(queue, hk, piece, "hk") for queue, piece in zip((nc.scalar, nc.sync), HK_PIECES)]
-        nc.sync.dma_start(
-            out=pool_words[:],
-            in_=keys_words[0].rearrange("p n t -> p (n t)").bitcast(I32),
-        )
-        query_raw = tile([P, PACK, Q], F32, "query_raw")
-        nc.sync.dma_start(out=query_raw[:], in_=query.rearrange("(p t) q -> p t q", t=PACK))
-        hq_raw = [load_piece(nc.sync, hq, piece, "hq") for piece in HQ_PIECES]
-
-        warm_in = tile([P, 8], F32, "warm_in")
-        warm_out = tile([P, 8], F32, "warm_out")
-        nc.vector.memset(warm_in[:], 0.0)
-        nc.scalar.activation(warm_out[:], warm_in[:], ACT.Exp)
 
         def deal(copy, raw, dealt):
             copy(
@@ -74,17 +79,38 @@ def tile_attend_rotatedscores_kernel(tc, query, hq, hk, keys_words, keys_scales,
                 in_=raw.rearrange("p t (u j i) -> p u j t i", j=PACK, i=4),
             )
 
+        def quantize(codes, scales, values):
+            nc.vector.quantize_mx(out=codes.bitcast(FP8X4), scales=scales, in_=values)
+
+        def product(bank, lhs_codes, lhs_scales, rhs_codes, rhs_scales):
+            nc.tensor.matmul_mx(
+                out=bank,
+                lhsT=lhs_codes.bitcast(FP8X4),
+                lhsT_scale=lhs_scales,
+                rhs=rhs_codes.bitcast(FP8X4),
+                rhs_scale=rhs_scales,
+                start=True,
+                stop=True,
+            )
+
         hk_dealt = tile([P, PACK, D], BF16, "hk_dealt")
-        deal(nc.scalar.copy, hk_raw[0][:], hk_dealt[:, :, HK_PIECES[0][0] : HK_PIECES[0][1]])
-        deal(nc.vector.tensor_copy, hk_raw[1][:], hk_dealt[:, :, HK_PIECES[1][0] : HK_PIECES[1][1]])
-
-
+        deal(nc.scalar.copy, hk_raw[:, :, :HK_SCALAR_COLS], hk_dealt[:, :, :HK_SCALAR_COLS])
+        deal(nc.vector.tensor_copy, hk_raw[:, :, HK_SCALAR_COLS:], hk_dealt[:, :, HK_SCALAR_COLS:])
         hk_codes = tile([P, D], U32, "hk_codes")
         hk_scales = tile([P, D], U8, "hk_scales")
-        nc.vector.quantize_mx(
-            out=hk_codes[:].bitcast(FP8X4), scales=hk_scales[:], in_=hk_dealt[:].rearrange("p j x -> p (j x)")
-        )
+        quantize(hk_codes[:], hk_scales[:], hk_dealt[:].rearrange("p j x -> p (j x)"))
 
+        hq_codes = [tile([P, P], U32, "hq_codes%d" % j) for j in range(PACK)]
+        hq_scales = [tile([P, P], U8, "hq_scales%d" % j) for j in range(PACK)]
+
+        def quantize_hq(half):
+            dealt = tile([P, PACK, D // 2], BF16, "hq_dealt%d" % half)
+            deal(nc.vector.tensor_copy, hq_raw[half][:], dealt[:])
+            cols = slice(half * (P // 2), (half + 1) * (P // 2))
+            for j in range(PACK):
+                quantize(hq_codes[j][:, cols], hq_scales[j][:, cols], dealt[:, j, :])
+
+        quantize_hq(0)
         key_words = []
         for h in range(2):
             gathered = tile([P, I // 2], U32, "key_words%d" % h)
@@ -93,86 +119,54 @@ def tile_attend_rotatedscores_kernel(tc, query, hq, hk, keys_words, keys_scales,
             )
             key_words.append(gathered)
 
-        query_bf = tile([P, Q, PACK], BF16, "query_bf")
-        nc.scalar.copy(
-            out=query_bf[:].rearrange("p (c i) t -> p c t i", i=4),
-            in_=query_raw[:].rearrange("p t (c i) -> p c t i", i=4),
-        )
-
-        kr_bf = tile([P, I, PACK], BF16, "kr_bf")
+        kr_bf = tile([P, I - P, PACK], BF16, "kr_bf")
+        kr_banks = []
         for b in range(4):
             bank = ps.tile([P, PACK, P], F32, name="kr_bank%d" % b)
             cols = slice((b % 2) * P, (b % 2 + 1) * P)
             for j in range(PACK):
-                nc.tensor.matmul_mx(
-                    out=bank[:, j, :],
-                    lhsT=hk_codes[:, j * P : (j + 1) * P].bitcast(FP8X4),
-                    lhsT_scale=hk_scales[:, j * P : (j + 1) * P],
-                    rhs=key_words[b // 2][:, cols].bitcast(FP8X4),
-                    rhs_scale=key_scales[:, b * P : (b + 1) * P],
-                    start=True,
-                    stop=True,
+                product(
+                    bank[:, j, :],
+                    hk_codes[:, j * P : (j + 1) * P],
+                    hk_scales[:, j * P : (j + 1) * P],
+                    key_words[b // 2][:, cols],
+                    key_scales[:, b * P : (b + 1) * P],
                 )
-            nc.scalar.copy(out=kr_bf[:, b * P : (b + 1) * P, :], in_=bank[:].rearrange("p j n -> p n j"))
+            kr_banks.append(bank)
+            if b < 3:
+                nc.scalar.copy(out=kr_bf[:, b * P : (b + 1) * P, :], in_=bank[:].rearrange("p j n -> p n j"))
 
+
+        quantize_hq(1)
+        query_bf = tile([P, Q, PACK], BF16, "query_bf")
+        nc.vector.tensor_copy(
+            out=query_bf[:].rearrange("p (c i) t -> p c t i", i=4),
+            in_=query_raw[:].rearrange("p t (c i) -> p c t i", i=4),
+        )
         query_codes = tile([P, Q], U32, "query_codes")
         query_scales = tile([P, Q], U8, "query_scales")
-        nc.vector.quantize_mx(
-            out=query_codes[:].bitcast(FP8X4),
-            scales=query_scales[:],
-            in_=query_bf[:].rearrange("p q t -> p (q t)"),
-        )
-        hq_codes = [tile([P, P], U32, "hq_codes%d" % j) for j in range(PACK)]
-        hq_scales = [tile([P, P], U8, "hq_scales%d" % j) for j in range(PACK)]
-        for half in range(2):
-            dealt = tile([P, PACK, D // 2], BF16, "hq_dealt%d" % half)
-            base = half * (D // 2)
-            for raw, (lo, hi) in zip(hq_raw, HQ_PIECES):
-                if base <= lo < base + D // 2:
-                    deal(nc.vector.tensor_copy, raw[:], dealt[:, :, lo - base : hi - base])
-            cols = slice(half * (P // 2), (half + 1) * (P // 2))
-            for j in range(PACK):
-                nc.vector.quantize_mx(
-                    out=hq_codes[j][:, cols].bitcast(FP8X4), scales=hq_scales[j][:, cols], in_=dealt[:, j, :]
-                )
+        quantize(query_codes[:], query_scales[:], query_bf[:].rearrange("p q t -> p (q t)"))
+
+        kr_last_bf = tile([P, P, PACK], BF16, "kr_last_bf", tag="query_bf")
+        nc.vector.tensor_copy(kr_last_bf[:], kr_banks[3][:].rearrange("p j n -> p n j"))
 
         qr_bank = ps.tile([P, PACK, Q], F32, name="qr_bank")
         for j in range(PACK):
-            nc.tensor.matmul_mx(
-                out=qr_bank[:, j, :],
-                lhsT=hq_codes[j][:].bitcast(FP8X4),
-                lhsT_scale=hq_scales[j][:],
-                rhs=query_codes[:].bitcast(FP8X4),
-                rhs_scale=query_scales[:],
-                start=True,
-                stop=True,
-            )
+            product(qr_bank[:, j, :], hq_codes[j][:], hq_scales[j][:], query_codes[:], query_scales[:])
         qr_bf = tile([P, Q, PACK], BF16, "qr_bf")
         nc.scalar.copy(out=qr_bf[:], in_=qr_bank[:].rearrange("p j n -> p n j"))
 
         kr_codes = tile([P, I], U32, "kr_codes", tag="hq_dealt1")
         kr_scales = tile([P, I], U8, "kr_scales")
-        nc.vector.quantize_mx(
-            out=kr_codes[:].bitcast(FP8X4), scales=kr_scales[:], in_=kr_bf[:].rearrange("p n j -> p (n j)")
-        )
+        for lo, hi in ((0, 2 * P), (2 * P, 3 * P)):
+            quantize(kr_codes[:, lo:hi], kr_scales[:, lo:hi], kr_bf[:, lo:hi, :].rearrange("p n j -> p (n j)"))
+        quantize(kr_codes[:, 3 * P :], kr_scales[:, 3 * P :], kr_last_bf[:].rearrange("p n j -> p (n j)"))
         qr_codes = tile([P, Q], U32, "qr_codes")
         qr_scales = tile([P, Q], U8, "qr_scales")
-        nc.vector.quantize_mx(
-            out=qr_codes[:].bitcast(FP8X4),
-            scales=qr_scales[:],
-            in_=qr_bf[:].rearrange("p q j -> p (q j)"),
-        )
+        quantize(qr_codes[:], qr_scales[:], qr_bf[:].rearrange("p q j -> p (q j)"))
 
         scores = ps.tile([P, I], F32, name="scores")
-        nc.tensor.matmul_mx(
-            out=scores[:],
-            lhsT=qr_codes[:].bitcast(FP8X4),
-            lhsT_scale=qr_scales[:],
-            rhs=kr_codes[:].bitcast(FP8X4),
-            rhs_scale=kr_scales[:],
-            start=True,
-            stop=True,
-        )
+        product(scores[:], qr_codes[:], qr_scales[:], kr_codes[:], kr_scales[:])
         neg_max = tile([P, 1], F32, "neg_max")
         nc.vector.tensor_reduce(neg_max[:], scores[:], AX.X, ALU.max, negate=True)
         weights = tile([P, I], F32, "weights")

@@ -111,6 +111,9 @@ def tile_attend_rotatedscores_kernel(tc, query, hq, hk, keys_words, keys_scales,
                 quantize(hq_codes[j][:, cols], hq_scales[j][:, cols], dealt[:, j, :])
 
         quantize_hq(0)
+        warm_bank = ps.tile([P, I], F32, name="warm_bank")
+        for width in (I, 256):
+            product(warm_bank[:, :width], hk_codes[:, :P], hk_scales[:, :P], pool_words[:, :width], key_scales[:, :width])
         key_words = []
         for h in range(2):
             gathered = tile([P, I // 2], U32, "key_words%d" % h)

@@ -59,8 +59,8 @@ def tile_attend_rotatedscores_kernel(tc, query, hq, hk, keys_words, keys_scales,
         nc.sync.dma_start(out=hk_raw[:, 2:4, :], in_=hk_rows[:, 2:4, :])
         load_hq(0)
         load_words()
-        load_hq(1)
         nc.sync.dma_start(out=query_raw[:], in_=query.rearrange("(p t) q -> p t q", t=PACK))
+        load_hq(1)
 
         warm_in = tile([P, 8], F32, "warm_in")
         warm_out = tile([P, 8], F32, "warm_out")
@@ -122,6 +122,15 @@ def tile_attend_rotatedscores_kernel(tc, query, hq, hk, keys_words, keys_scales,
             )
             key_words.append(gathered)
 
+        query_bf = tile([P, Q, PACK], BF16, "query_bf")
+        nc.scalar.copy(
+            out=query_bf[:].rearrange("p (c i) t -> p c t i", i=4),
+            in_=query_raw[:].rearrange("p t (c i) -> p c t i", i=4),
+        )
+        query_codes = tile([P, Q], U32, "query_codes")
+        query_scales = tile([P, Q], U8, "query_scales")
+        quantize(query_codes[:], query_scales[:], query_bf[:].rearrange("p q t -> p (q t)"))
+
         kr_bf = tile([P, I - P, PACK], BF16, "kr_bf")
         kr_banks = []
         for b in range(4):
@@ -139,18 +148,19 @@ def tile_attend_rotatedscores_kernel(tc, query, hq, hk, keys_words, keys_scales,
             if b < 3:
                 nc.scalar.copy(out=kr_bf[:, b * P : (b + 1) * P, :], in_=bank[:].rearrange("p j n -> p n j"))
 
+        late_places = ((0, 2), (2, 3), (3, 4))
+        late_dealt = []
+        for lo, hi in late_places:
+            dealt = tile([P, hi - lo, D // 2], BF16, "hq_late%d" % lo)
+            nc.vector.tensor_copy(
+                out=dealt[:].rearrange("p j (u i t) -> p u j t i", i=4, t=PACK),
+                in_=hq_raw[1][:].rearrange("p t (u j i) -> p u j t i", j=PACK, i=4)[:, :, lo:hi],
+            )
+            late_dealt += [dealt[:, j, :] for j in range(hi - lo)]
+        for j in range(PACK):
+            quantize(hq_codes[j][:, P // 2 :], hq_scales[j][:, P // 2 :], late_dealt[j])
 
-        quantize_hq(1)
-        query_bf = tile([P, Q, PACK], BF16, "query_bf")
-        nc.vector.tensor_copy(
-            out=query_bf[:].rearrange("p (c i) t -> p c t i", i=4),
-            in_=query_raw[:].rearrange("p t (c i) -> p c t i", i=4),
-        )
-        query_codes = tile([P, Q], U32, "query_codes")
-        query_scales = tile([P, Q], U8, "query_scales")
-        quantize(query_codes[:], query_scales[:], query_bf[:].rearrange("p q t -> p (q t)"))
-
-        kr_last_bf = tile([P, P, PACK], BF16, "kr_last_bf", tag="query_bf")
+        kr_last_bf = tile([P, P, PACK], BF16, "kr_last_bf", tag="hq_late0")
         nc.vector.tensor_copy(kr_last_bf[:], kr_banks[3][:].rearrange("p j n -> p n j"))
 
         qr_bank = ps.tile([P, PACK, Q], F32, name="qr_bank")
@@ -159,7 +169,7 @@ def tile_attend_rotatedscores_kernel(tc, query, hq, hk, keys_words, keys_scales,
         qr_bf = tile([P, Q, PACK], BF16, "qr_bf")
         nc.scalar.copy(out=qr_bf[:], in_=qr_bank[:].rearrange("p j n -> p n j"))
 
-        kr_codes = tile([P, I], U32, "kr_codes", tag="hq_dealt1")
+        kr_codes = tile([P, I], U32, "kr_codes", tag="hq_late3")
         kr_scales = tile([P, I], U8, "kr_scales")
         for lo, hi in ((0, 2 * P), (2 * P, 3 * P)):
             quantize(kr_codes[:, lo:hi], kr_scales[:, lo:hi], kr_bf[:, lo:hi, :].rearrange("p n j -> p (n j)"))

@@ -113,7 +113,7 @@ def tile_attend_rotatedscores_kernel(tc, query, hq, hk, keys_words, keys_scales,
         quantize_hq(0)
         warm_bank = ps.tile([P, I], F32, name="warm_bank")
         for width in (I, 256):
-            product(warm_bank[:, :width], hk_codes[:, :P], hk_scales[:, :P], pool_words[:, :width], key_scales[:, :width])
+            product(warm_bank[:, :width], hk_codes[:, :P], hk_scales[:, :P], hk_codes[:, :width], hk_scales[:, :width])
         key_words = []
         for h in range(2):
             gathered = tile([P, I // 2], U32, "key_words%d" % h)

@@ -18,65 +18,27 @@ AX = mybir.AxisListType
 
 P = 128
 PACK = 4
-HK_SCALAR_COLS = 384
+HALF = D // 2
+HK_SCALAR_COLS = 320
 
 
 def tile_attend_rotatedscores_kernel(tc, query, hq, hk, keys_words, keys_scales, offs, out):
     nc = tc.nc
     with ExitStack() as ctx:
         sb = ctx.enter_context(tc.tile_pool(name="sb", bufs=1))
+        reused = ctx.enter_context(tc.tile_pool(name="reused", bufs=1))
         ps = ctx.enter_context(tc.psum_pool(name="ps", bufs=1))
 
         def tile(shape, dtype, name, tag=None):
             return sb.tile(shape, dtype, name=name, tag=tag or name, align_bytes=64)
 
-        offsets = sb.tile([P, I // 16], U16, name="offsets")
-        pool_scales = tile([P, T], U8, "pool_scales")
-        pool_words = tile([P, T], I32, "pool_words")
-        scale_rows = tile([P, T // 4], I32, "scale_rows")
-        hk_raw = tile([P, PACK, D], F32, "hk_raw")
-        hq_raw = [tile([P, PACK, D // 2], F32, "hq_raw%d" % half) for half in range(2)]
-        query_raw = tile([P, PACK, Q], F32, "query_raw")
-        hk_rows = hk.rearrange("(p t) d -> p t d", t=PACK)
-        hq_rows = hq.rearrange("(p t) d -> p t d", t=PACK)
+        def tile_at(offset, shape, dtype, name):
+            return reused.tile(shape, dtype, name=name, align_bytes=64, offset=offset)
 
-        def load_scales(queue, quad):
-            queue.dma_start(
-                out=scale_rows[32 * quad : 32 * quad + 4, :],
-                in_=keys_scales[0, 4 * quad : 4 * quad + 4, :].bitcast(I32),
-            )
-
-        def load_hq(half):
-            nc.sync.dma_start(out=hq_raw[half][:], in_=hq_rows[:, :, half * (D // 2) : (half + 1) * (D // 2)])
-
-        def load_words():
-            nc.sync.dma_start(out=pool_words[:], in_=keys_words[0].rearrange("p n t -> p (n t)").bitcast(I32))
-
-        nc.scalar.dma_start(out=hk_raw[:, 0:2, :], in_=hk_rows[:, 0:2, :])
-        for quad in (0, 2, 1, 3):
-            load_scales(nc.sync, quad)
-        nc.sync.dma_start(offsets[:], offs)
-        nc.sync.dma_start(out=hk_raw[:, 2:4, :], in_=hk_rows[:, 2:4, :])
-        load_hq(0)
-        load_words()
-        nc.sync.dma_start(out=query_raw[:], in_=query.rearrange("(p t) q -> p t q", t=PACK))
-        load_hq(1)
-
-        warm_in = tile([P, 8], F32, "warm_in")
-        warm_out = tile([P, 8], F32, "warm_out")
-        nc.gpsimd.memset(warm_in[:], 0.0)
-        nc.scalar.activation(warm_out[:], warm_in[:], ACT.Exp)
-        nc.vector.memset(pool_scales[:].bitcast(I32), 0)
-        for quad in (0, 2, 1, 3):
-            rows = slice(32 * quad, 32 * quad + 4)
-            nc.vector.tensor_copy(pool_scales[:].bitcast(I32)[rows, :], scale_rows[rows, :])
-        key_scales = tile([P, I], U8, "key_scales")
-        nc.vector.tensor_copy(key_scales[:], pool_scales[:].indirect(offsets[:]))
-
-        def deal(copy, raw, dealt):
+        def deal(copy, raw, dealt, places):
             copy(
                 out=dealt.rearrange("p j (u i t) -> p u j t i", i=4, t=PACK),
-                in_=raw.rearrange("p t (u j i) -> p u j t i", j=PACK, i=4),
+                in_=raw.rearrange("p t (u j i) -> p u j t i", j=PACK, i=4)[:, :, places],
             )
 
         def quantize(codes, scales, values):
@@ -93,34 +55,53 @@ def tile_attend_rotatedscores_kernel(tc, query, hq, hk, keys_words, keys_scales,
                 stop=True,
             )
 
-        hk_dealt = tile([P, PACK, D], BF16, "hk_dealt")
-        deal(nc.scalar.copy, hk_raw[:, :, :HK_SCALAR_COLS], hk_dealt[:, :, :HK_SCALAR_COLS])
-        deal(nc.vector.tensor_copy, hk_raw[:, :, HK_SCALAR_COLS:], hk_dealt[:, :, HK_SCALAR_COLS:])
-        hk_codes = tile([P, D], U32, "hk_codes")
-        hk_scales = tile([P, D], U8, "hk_scales")
-        quantize(hk_codes[:], hk_scales[:], hk_dealt[:].rearrange("p j x -> p (j x)"))
+        offsets = sb.tile([P, I // 16], U16, name="offsets")
+        pool_scales = tile_at(8192, [P, T], U8, "pool_scales")
+        pool_words = tile_at(0, [P, T], I32, "pool_words")
+        hk_raw = tile([P, PACK, D], F32, "hk_raw")
+        hq_raw = [tile([P, PACK, HALF], F32, "hq_raw%d" % half) for half in range(2)]
+        query_raw = tile([P, PACK, Q], F32, "query_raw")
+        hk_rows = hk.rearrange("(p t) d -> p t d", t=PACK)
+        hq_rows = hq.rearrange("(p t) d -> p t d", t=PACK)
 
-        hq_codes = [tile([P, P], U32, "hq_codes%d" % j) for j in range(PACK)]
-        hq_scales = [tile([P, P], U8, "hq_scales%d" % j) for j in range(PACK)]
-
-        def quantize_hq(half):
-            dealt = tile([P, PACK, D // 2], BF16, "hq_dealt%d" % half)
-            deal(nc.vector.tensor_copy, hq_raw[half][:], dealt[:])
-            cols = slice(half * (P // 2), (half + 1) * (P // 2))
-            for j in range(PACK):
-                quantize(hq_codes[j][:, cols], hq_scales[j][:, cols], dealt[:, j, :])
-
-        quantize_hq(0)
-        warm_bank = ps.tile([P, I], F32, name="warm_bank")
-        for width in (I, 256):
-            product(warm_bank[:, :width], hk_codes[:, :P], hk_scales[:, :P], hk_codes[:, :width], hk_scales[:, :width])
-        key_words = []
-        for h in range(2):
-            gathered = tile([P, I // 2], U32, "key_words%d" % h)
-            nc.vector.tensor_copy(
-                gathered[:], pool_words[:].bitcast(U32).indirect(offsets[:, 16 * h : 16 * (h + 1)])
+        nc.vector.memset(pool_scales[:].bitcast(I32)[:, : 384], 0)
+        nc.gpsimd.memset(pool_scales[:].bitcast(I32)[:, 384 :], 0)
+        for pair in range(2):
+            nc.sync.dma_start(out=hk_raw[:, 2 * pair : 2 * pair + 2, :], in_=hk_rows[:, 2 * pair : 2 * pair + 2, :])
+        nc.sync.dma_start(offsets[:], offs)
+        for row in range(4):
+            nc.sync.dma_start(
+                out=pool_scales[:].bitcast(I32)[row:P:32, :],
+                in_=keys_scales[0].rearrange("(g r) n -> r g n", r=4)[row].bitcast(I32),
             )
-            key_words.append(gathered)
+        nc.sync.dma_start(out=pool_words[:], in_=keys_words[0].rearrange("p n t -> p (n t)").bitcast(I32))
+        nc.sync.dma_start(out=query_raw[:], in_=query.rearrange("(p t) q -> p t q", t=PACK))
+        for half in range(2):
+            nc.sync.dma_start(out=hq_raw[half][:], in_=hq_rows[:, :, half * HALF : (half + 1) * HALF])
+
+        warm_in = tile([P, 8], F32, "warm_in")
+        warm_out = tile([P, 8], F32, "warm_out")
+        nc.vector.memset(warm_in[:], 0.0)
+        nc.scalar.activation(warm_out[:], warm_in[:], ACT.Exp)
+
+        hk_dealt = tile([P, PACK, D], BF16, "hk_dealt")
+        every = slice(0, PACK)
+        deal(nc.scalar.copy, hk_raw[:, :, :HK_SCALAR_COLS], hk_dealt[:, :, :HK_SCALAR_COLS], every)
+        deal(nc.vector.tensor_copy, hk_raw[:, :, HK_SCALAR_COLS:], hk_dealt[:, :, HK_SCALAR_COLS:], every)
+        key_scales = tile([P, I], U8, "key_scales")
+        nc.vector.tensor_copy(key_scales[:], pool_scales[:].indirect(offsets[:]))
+        hk_codes = tile([P, D], U32, "hk_codes")
+        hk_scales = tile_at(8192, [P, D], U8, "hk_scales")
+        quantize(hk_codes[:], hk_scales[:], hk_dealt[:].rearrange("p j x -> p (j x)"))
+        warm_bank = ps.tile([P, I], F32, name="warm_bank")
+        for rows in (slice(0, 64), slice(64, 128)):
+            product(warm_bank[:64, :], hk_codes[:, rows], hk_scales[:, rows], hk_codes[:], hk_scales[:])
+        key_words = tile_at(8192 + 512, [P, I], U32, "key_words")
+        for h in range(2):
+            nc.vector.tensor_copy(
+                key_words[:, h * (I // 2) : (h + 1) * (I // 2)],
+                pool_words[:].bitcast(U32).indirect(offsets[:, 16 * h : 16 * (h + 1)]),
+            )
 
         query_bf = tile([P, Q, PACK], BF16, "query_bf")
         nc.scalar.copy(
@@ -131,55 +112,53 @@ def tile_attend_rotatedscores_kernel(tc, query, hq, hk, keys_words, keys_scales,
         query_scales = tile([P, Q], U8, "query_scales")
         quantize(query_codes[:], query_scales[:], query_bf[:].rearrange("p q t -> p (q t)"))
 
-        kr_bf = tile([P, I - P, PACK], BF16, "kr_bf")
-        kr_banks = []
+        kr_bf = tile([P, I, PACK], BF16, "kr_bf", tag="query_raw")
         for b in range(4):
             bank = ps.tile([P, PACK, P], F32, name="kr_bank%d" % b)
-            cols = slice((b % 2) * P, (b % 2 + 1) * P)
             for j in range(PACK):
                 product(
                     bank[:, j, :],
                     hk_codes[:, j * P : (j + 1) * P],
                     hk_scales[:, j * P : (j + 1) * P],
-                    key_words[b // 2][:, cols],
+                    key_words[:, b * P : (b + 1) * P],
                     key_scales[:, b * P : (b + 1) * P],
                 )
-            kr_banks.append(bank)
-            if b < 3:
-                nc.scalar.copy(out=kr_bf[:, b * P : (b + 1) * P, :], in_=bank[:].rearrange("p j n -> p n j"))
+            nc.scalar.copy(out=kr_bf[:, b * P : (b + 1) * P, :], in_=bank[:].rearrange("p j n -> p n j"))
 
-        late_places = ((0, 2), (2, 3), (3, 4))
-        late_dealt = []
-        for lo, hi in late_places:
-            dealt = tile([P, hi - lo, D // 2], BF16, "hq_late%d" % lo)
-            nc.vector.tensor_copy(
-                out=dealt[:].rearrange("p j (u i t) -> p u j t i", i=4, t=PACK),
-                in_=hq_raw[1][:].rearrange("p t (u j i) -> p u j t i", j=PACK, i=4)[:, :, lo:hi],
-            )
-            late_dealt += [dealt[:, j, :] for j in range(hi - lo)]
+        hq_codes = [tile([P, P], U32, "hq_codes%d" % j) for j in range(PACK)]
+        hq_scales = [tile([P, P], U8, "hq_scales%d" % j) for j in range(PACK)]
+        for half in range(2):
+            dealt = []
+            for lo, hi in ((0, 2), (2, 3), (3, 4)):
+                group = tile_at(12288 + 2048 * half + 512 * lo, [P, hi - lo, HALF], BF16, "hq_dealt%d%d" % (half, lo))
+                deal(nc.vector.tensor_copy, hq_raw[half][:], group[:], slice(lo, hi))
+                dealt += [group[:, j, :] for j in range(hi - lo)]
+            cols = slice(half * (P // 2), (half + 1) * (P // 2))
+            for j in range(PACK):
+                quantize(hq_codes[j][:, cols], hq_scales[j][:, cols], dealt[j])
+
+        qr_banks = [ps.tile([P, PACK, Q // 2], F32, name="qr_bank%d" % h) for h in range(2)]
         for j in range(PACK):
-            quantize(hq_codes[j][:, P // 2 :], hq_scales[j][:, P // 2 :], late_dealt[j])
-
-        kr_last_bf = tile([P, P, PACK], BF16, "kr_last_bf", tag="hq_late0")
-        nc.vector.tensor_copy(kr_last_bf[:], kr_banks[3][:].rearrange("p j n -> p n j"))
-
-        qr_bank = ps.tile([P, PACK, Q], F32, name="qr_bank")
-        for j in range(PACK):
-            product(qr_bank[:, j, :], hq_codes[j][:], hq_scales[j][:], query_codes[:], query_scales[:])
+            for h in range(2):
+                rows = slice(h * (Q // 2), (h + 1) * (Q // 2))
+                product(qr_banks[h][:, j, :], hq_codes[j][:], hq_scales[j][:], query_codes[:, rows], query_scales[:, rows])
         qr_bf = tile([P, Q, PACK], BF16, "qr_bf")
-        nc.scalar.copy(out=qr_bf[:], in_=qr_bank[:].rearrange("p j n -> p n j"))
+        for h, copy in enumerate((nc.vector.tensor_copy, nc.scalar.copy)):
+            copy(out=qr_bf[:, h * (Q // 2) : (h + 1) * (Q // 2), :], in_=qr_banks[h][:].rearrange("p j n -> p n j"))
 
-        kr_codes = tile([P, I], U32, "kr_codes", tag="hq_late3")
+        kr_early = tile_at(12288 + 2048 + 512 * 3, [P, 3 * P], U32, "kr_early")
+        kr_last = tile([P, P], U32, "kr_last", tag="query_codes")
         kr_scales = tile([P, I], U8, "kr_scales")
-        for lo, hi in ((0, 2 * P), (2 * P, 3 * P)):
-            quantize(kr_codes[:, lo:hi], kr_scales[:, lo:hi], kr_bf[:, lo:hi, :].rearrange("p n j -> p (n j)"))
-        quantize(kr_codes[:, 3 * P :], kr_scales[:, 3 * P :], kr_last_bf[:].rearrange("p n j -> p (n j)"))
+        kr_parts = [(kr_early[:, : 2 * P], slice(0, 2 * P)), (kr_early[:, 2 * P :], slice(2 * P, 3 * P)), (kr_last[:], slice(3 * P, I))]
+        for codes, slots in kr_parts:
+            quantize(codes, kr_scales[:, slots], kr_bf[:, slots, :].rearrange("p n j -> p (n j)"))
         qr_codes = tile([P, Q], U32, "qr_codes")
         qr_scales = tile([P, Q], U8, "qr_scales")
         quantize(qr_codes[:], qr_scales[:], qr_bf[:].rearrange("p q j -> p (q j)"))
 
         scores = ps.tile([P, I], F32, name="scores")
-        product(scores[:], qr_codes[:], qr_scales[:], kr_codes[:], kr_scales[:])
+        for codes, slots in kr_parts:
+            product(scores[:, slots], qr_codes[:], qr_scales[:], codes, kr_scales[:, slots])
         neg_max = tile([P, 1], F32, "neg_max")
         nc.vector.tensor_reduce(neg_max[:], scores[:], AX.X, ALU.max, negate=True)
         weights = tile([P, I], F32, "weights")

@@ -64,15 +64,14 @@ def tile_attend_rotatedscores_kernel(tc, query, hq, hk, keys_words, keys_scales,
         hk_rows = hk.rearrange("(p t) d -> p t d", t=PACK)
         hq_rows = hq.rearrange("(p t) d -> p t d", t=PACK)
 
-        nc.vector.memset(pool_scales[:].bitcast(I32)[:, : 384], 0)
-        nc.gpsimd.memset(pool_scales[:].bitcast(I32)[:, 384 :], 0)
-        for pair in range(2):
-            nc.sync.dma_start(out=hk_raw[:, 2 * pair : 2 * pair + 2, :], in_=hk_rows[:, 2 * pair : 2 * pair + 2, :])
+        nc.vector.memset(pool_scales[:].bitcast(I32), 0)
         nc.sync.dma_start(offsets[:], offs)
-        for row in range(4):
+        nc.scalar.dma_start(out=hk_raw[:, 0:3, :], in_=hk_rows[:, 0:3, :])
+        nc.sync.dma_start(out=hk_raw[:, 3:4, :], in_=hk_rows[:, 3:4, :])
+        for quad in (0, 2, 1, 3):
             nc.sync.dma_start(
-                out=pool_scales[:].bitcast(I32)[row:P:32, :],
-                in_=keys_scales[0].rearrange("(g r) n -> r g n", r=4)[row].bitcast(I32),
+                out=pool_scales[:].bitcast(I32)[32 * quad : 32 * quad + 4, :],
+                in_=keys_scales[0, 4 * quad : 4 * quad + 4, :].bitcast(I32),
             )
         nc.sync.dma_start(out=pool_words[:], in_=keys_words[0].rearrange("p n t -> p (n t)").bitcast(I32))
         nc.sync.dma_start(out=query_raw[:], in_=query.rearrange("(p t) q -> p t q", t=PACK))
@@ -94,9 +93,7 @@ def tile_attend_rotatedscores_kernel(tc, query, hq, hk, keys_words, keys_scales,
         hk_scales = tile_at(8192, [P, D], U8, "hk_scales")
         quantize(hk_codes[:], hk_scales[:], hk_dealt[:].rearrange("p j x -> p (j x)"))
         warm_bank = ps.tile([P, I], F32, name="warm_bank")
-        for rows in (slice(0, 64), slice(64, 128)):
-            product(warm_bank[:64, :], hk_codes[:, rows], hk_scales[:, rows], hk_codes[:], hk_scales[:])
-        key_words = tile_at(8192 + 512, [P, I], U32, "key_words")
+        key_words = tile_at(8192 + 1024, [P, I], U32, "key_words")
         for h in range(2):
             nc.vector.tensor_copy(
                 key_words[:, h * (I // 2) : (h + 1) * (I // 2)],
@@ -125,6 +122,8 @@ def tile_attend_rotatedscores_kernel(tc, query, hq, hk, keys_words, keys_scales,
                 )
             nc.scalar.copy(out=kr_bf[:, b * P : (b + 1) * P, :], in_=bank[:].rearrange("p j n -> p n j"))
 
+        product(warm_bank[:, :256], hk_codes[:, :P], hk_scales[:, :P], key_words[:, 256:], key_scales[:, 256:])
+
         hq_codes = [tile([P, P], U32, "hq_codes%d" % j) for j in range(PACK)]
         hq_scales = [tile([P, P], U8, "hq_scales%d" % j) for j in range(PACK)]
         for half in range(2):
@@ -137,28 +136,23 @@ def tile_attend_rotatedscores_kernel(tc, query, hq, hk, keys_words, keys_scales,
             for j in range(PACK):
                 quantize(hq_codes[j][:, cols], hq_scales[j][:, cols], dealt[j])
 
-        qr_banks = [ps.tile([P, PACK, Q // 2], F32, name="qr_bank%d" % h) for h in range(2)]
+        qr_bank = ps.tile([P, PACK, Q], F32, name="qr_bank")
         for j in range(PACK):
-            for h in range(2):
-                rows = slice(h * (Q // 2), (h + 1) * (Q // 2))
-                product(qr_banks[h][:, j, :], hq_codes[j][:], hq_scales[j][:], query_codes[:, rows], query_scales[:, rows])
+            product(qr_bank[:, j, :], hq_codes[j][:], hq_scales[j][:], query_codes[:], query_scales[:])
+        product(warm_bank[:], hq_codes[3][:], hq_scales[3][:], key_words[:], key_scales[:])
         qr_bf = tile([P, Q, PACK], BF16, "qr_bf")
-        for h, copy in enumerate((nc.vector.tensor_copy, nc.scalar.copy)):
-            copy(out=qr_bf[:, h * (Q // 2) : (h + 1) * (Q // 2), :], in_=qr_banks[h][:].rearrange("p j n -> p n j"))
+        nc.scalar.copy(out=qr_bf[:], in_=qr_bank[:].rearrange("p j n -> p n j"))
 
-        kr_early = tile_at(12288 + 2048 + 512 * 3, [P, 3 * P], U32, "kr_early")
-        kr_last = tile([P, P], U32, "kr_last", tag="query_codes")
+        kr_codes = tile_at(12288 + 2048 + 512 * 3, [P, I], U32, "kr_codes")
         kr_scales = tile([P, I], U8, "kr_scales")
-        kr_parts = [(kr_early[:, : 2 * P], slice(0, 2 * P)), (kr_early[:, 2 * P :], slice(2 * P, 3 * P)), (kr_last[:], slice(3 * P, I))]
-        for codes, slots in kr_parts:
-            quantize(codes, kr_scales[:, slots], kr_bf[:, slots, :].rearrange("p n j -> p (n j)"))
+        for slots in (slice(0, I // 2), slice(I // 2, I)):
+            quantize(kr_codes[:, slots], kr_scales[:, slots], kr_bf[:, slots, :].rearrange("p n j -> p (n j)"))
         qr_codes = tile([P, Q], U32, "qr_codes")
         qr_scales = tile([P, Q], U8, "qr_scales")
         quantize(qr_codes[:], qr_scales[:], qr_bf[:].rearrange("p q j -> p (q j)"))
 
         scores = ps.tile([P, I], F32, name="scores")
-        for codes, slots in kr_parts:
-            product(scores[:, slots], qr_codes[:], qr_scales[:], codes, kr_scales[:, slots])
+        product(scores[:], qr_codes[:], qr_scales[:], kr_codes[:], kr_scales[:])
         neg_max = tile([P, 1], F32, "neg_max")
         nc.vector.tensor_reduce(neg_max[:], scores[:], AX.X, ALU.max, negate=True)
         weights = tile([P, I], F32, "weights")

@@ -66,8 +66,8 @@ def tile_attend_rotatedscores_kernel(tc, query, hq, hk, keys_words, keys_scales,
 
         nc.vector.memset(pool_scales[:].bitcast(I32), 0)
         nc.sync.dma_start(offsets[:], offs)
-        nc.scalar.dma_start(out=hk_raw[:, 0:3, :], in_=hk_rows[:, 0:3, :])
-        nc.sync.dma_start(out=hk_raw[:, 3:4, :], in_=hk_rows[:, 3:4, :])
+        nc.scalar.dma_start(out=hk_raw[:, 0:2, :], in_=hk_rows[:, 0:2, :])
+        nc.sync.dma_start(out=hk_raw[:, 2:4, :], in_=hk_rows[:, 2:4, :])
         for quad in (0, 2, 1, 3):
             nc.sync.dma_start(
                 out=pool_scales[:].bitcast(I32)[32 * quad : 32 * quad + 4, :],

@@ -19,7 +19,9 @@ AX = mybir.AxisListType
 P = 128
 PACK = 4
 HALF = D // 2
-HK_SCALAR_COLS = 320
+HK_SCALAR_COLS = 192
+SCALE_ROW0 = P - 16
+WARM_ROWS = 32
 
 
 def tile_attend_rotatedscores_kernel(tc, query, hq, hk, keys_words, keys_scales, offs, out):
@@ -56,25 +58,33 @@ def tile_attend_rotatedscores_kernel(tc, query, hq, hk, keys_words, keys_scales,
             )
 
         offsets = sb.tile([P, I // 16], U16, name="offsets")
-        pool_scales = tile_at(8192, [P, T], U8, "pool_scales")
+        pool_scales = tile_at(16384, [P, T], U8, "pool_scales")
         pool_words = tile_at(0, [P, T], I32, "pool_words")
         hk_raw = tile([P, PACK, D], F32, "hk_raw")
-        hq_raw = [tile([P, PACK, HALF], F32, "hq_raw%d" % half) for half in range(2)]
         query_raw = tile([P, PACK, Q], F32, "query_raw")
         hk_rows = hk.rearrange("(p t) d -> p t d", t=PACK)
         hq_rows = hq.rearrange("(p t) d -> p t d", t=PACK)
 
-        nc.vector.memset(pool_scales[:].bitcast(I32), 0)
+        nc.vector.memset(pool_scales[:].bitcast(I32)[:SCALE_ROW0, :], 0)
         nc.sync.dma_start(offsets[:], offs)
+        nc.sync.dma_start(out=pool_scales[:].bitcast(I32)[SCALE_ROW0:, :], in_=keys_scales[0].bitcast(I32))
         nc.scalar.dma_start(out=hk_raw[:, 0:2, :], in_=hk_rows[:, 0:2, :])
         nc.sync.dma_start(out=hk_raw[:, 2:4, :], in_=hk_rows[:, 2:4, :])
-        for quad in (0, 2, 1, 3):
-            nc.sync.dma_start(
-                out=pool_scales[:].bitcast(I32)[32 * quad : 32 * quad + 4, :],
-                in_=keys_scales[0, 4 * quad : 4 * quad + 4, :].bitcast(I32),
-            )
         nc.sync.dma_start(out=pool_words[:], in_=keys_words[0].rearrange("p n t -> p (n t)").bitcast(I32))
         nc.sync.dma_start(out=query_raw[:], in_=query.rearrange("(p t) q -> p t q", t=PACK))
+        picked_scales = tile([P, I], U8, "picked_scales")
+        nc.vector.tensor_copy(picked_scales[:], pool_scales[:].indirect(offsets[:]))
+        key_scales = tile([P, I], U8, "key_scales")
+        nc.vector.memset(key_scales[:].bitcast(I32), 0)
+        for quad in range(4):
+            nc.sync.dma_start(
+                out=key_scales[:].bitcast(I32)[32 * quad : 32 * quad + 4, :],
+                in_=picked_scales[:].bitcast(I32)[SCALE_ROW0 + 4 * quad : SCALE_ROW0 + 4 * quad + 4, :],
+            )
+        hq_raw = [
+            tile_at(16384 + T - 128, [P, PACK, HALF], F32, "hq_raw0"),
+            tile_at(16384 + 1024 - 4096, [P, PACK, HALF], F32, "hq_raw1"),
+        ]
         for half in range(2):
             nc.sync.dma_start(out=hq_raw[half][:], in_=hq_rows[:, :, half * HALF : (half + 1) * HALF])
 
@@ -83,21 +93,19 @@ def tile_attend_rotatedscores_kernel(tc, query, hq, hk, keys_words, keys_scales,
         nc.vector.memset(warm_in[:], 0.0)
         nc.scalar.activation(warm_out[:], warm_in[:], ACT.Exp)
 
-        hk_dealt = tile([P, PACK, D], BF16, "hk_dealt")
+        hk_dealt = tile_at(8192, [P, PACK, D], BF16, "hk_dealt")
         every = slice(0, PACK)
         deal(nc.scalar.copy, hk_raw[:, :, :HK_SCALAR_COLS], hk_dealt[:, :, :HK_SCALAR_COLS], every)
         deal(nc.vector.tensor_copy, hk_raw[:, :, HK_SCALAR_COLS:], hk_dealt[:, :, HK_SCALAR_COLS:], every)
-        key_scales = tile([P, I], U8, "key_scales")
-        nc.vector.tensor_copy(key_scales[:], pool_scales[:].indirect(offsets[:]))
         hk_codes = tile([P, D], U32, "hk_codes")
-        hk_scales = tile_at(8192, [P, D], U8, "hk_scales")
+        hk_scales = tile_at(16384 + 1024, [P, D], U8, "hk_scales")
         quantize(hk_codes[:], hk_scales[:], hk_dealt[:].rearrange("p j x -> p (j x)"))
-        warm_bank = ps.tile([P, I], F32, name="warm_bank")
-        key_words = tile_at(8192 + 1024, [P, I], U32, "key_words")
-        for h in range(2):
+        warm_bank = ps.tile([WARM_ROWS, I], F32, name="warm_bank")
+        key_words = tile_at(8192, [P, I], U32, "key_words")
+        for b in range(4):
             nc.vector.tensor_copy(
-                key_words[:, h * (I // 2) : (h + 1) * (I // 2)],
-                pool_words[:].bitcast(U32).indirect(offsets[:, 16 * h : 16 * (h + 1)]),
+                key_words[:, b * P : (b + 1) * P],
+                pool_words[:].bitcast(U32).indirect(offsets[:, 8 * b : 8 * (b + 1)]),
             )
 
         query_bf = tile([P, Q, PACK], BF16, "query_bf")
@@ -122,14 +130,14 @@ def tile_attend_rotatedscores_kernel(tc, query, hq, hk, keys_words, keys_scales,
                 )
             nc.scalar.copy(out=kr_bf[:, b * P : (b + 1) * P, :], in_=bank[:].rearrange("p j n -> p n j"))
 
-        product(warm_bank[:, :256], hk_codes[:, :P], hk_scales[:, :P], key_words[:, 256:], key_scales[:, 256:])
+        product(warm_bank[:], hk_codes[:, :WARM_ROWS], hk_scales[:, :WARM_ROWS], key_words[:], key_scales[:])
 
         hq_codes = [tile([P, P], U32, "hq_codes%d" % j) for j in range(PACK)]
         hq_scales = [tile([P, P], U8, "hq_scales%d" % j) for j in range(PACK)]
         for half in range(2):
             dealt = []
             for lo, hi in ((0, 2), (2, 3), (3, 4)):
-                group = tile_at(12288 + 2048 * half + 512 * lo, [P, hi - lo, HALF], BF16, "hq_dealt%d%d" % (half, lo))
+                group = tile_at(24576 + 2048 * half + 512 * lo, [P, hi - lo, HALF], BF16, "hq_dealt%d%d" % (half, lo))
                 deal(nc.vector.tensor_copy, hq_raw[half][:], group[:], slice(lo, hi))
                 dealt += [group[:, j, :] for j in range(hi - lo)]
             cols = slice(half * (P // 2), (half + 1) * (P // 2))
@@ -139,11 +147,11 @@ def tile_attend_rotatedscores_kernel(tc, query, hq, hk, keys_words, keys_scales,
         qr_bank = ps.tile([P, PACK, Q], F32, name="qr_bank")
         for j in range(PACK):
             product(qr_bank[:, j, :], hq_codes[j][:], hq_scales[j][:], query_codes[:], query_scales[:])
-        product(warm_bank[:], hq_codes[3][:], hq_scales[3][:], key_words[:], key_scales[:])
+        product(warm_bank[:], hq_codes[3][:, :WARM_ROWS], hq_scales[3][:, :WARM_ROWS], key_words[:], key_scales[:])
         qr_bf = tile([P, Q, PACK], BF16, "qr_bf")
         nc.scalar.copy(out=qr_bf[:], in_=qr_bank[:].rearrange("p j n -> p n j"))
 
-        kr_codes = tile_at(12288 + 2048 + 512 * 3, [P, I], U32, "kr_codes")
+        kr_codes = tile_at(24576 + 2048 + 512 * 3, [P, I], U32, "kr_codes")
         kr_scales = tile([P, I], U8, "kr_scales")
         for slots in (slice(0, I // 2), slice(I // 2, I)):
             quantize(kr_codes[:, slots], kr_scales[:, slots], kr_bf[:, slots, :].rearrange("p n j -> p (n j)"))

@@ -67,7 +67,7 @@ def tile_attend_rotatedscores_kernel(tc, query, hq, hk, keys_words, keys_scales,
 
         nc.vector.memset(pool_scales[:].bitcast(I32)[:SCALE_ROW0, :], 0)
         nc.sync.dma_start(offsets[:], offs)
-        nc.sync.dma_start(out=pool_scales[:].bitcast(I32)[SCALE_ROW0:, :], in_=keys_scales[0].bitcast(I32))
+        nc.scalar.dma_start(out=pool_scales[:].bitcast(I32)[SCALE_ROW0:, :], in_=keys_scales[0].bitcast(I32))
         nc.scalar.dma_start(out=hk_raw[:, 0:2, :], in_=hk_rows[:, 0:2, :])
         nc.sync.dma_start(out=hk_raw[:, 2:4, :], in_=hk_rows[:, 2:4, :])
         nc.sync.dma_start(out=pool_words[:], in_=keys_words[0].rearrange("p n t -> p (n t)").bitcast(I32))

@@ -101,11 +101,12 @@ def tile_attend_rotatedscores_kernel(tc, query, hq, hk, keys_words, keys_scales,
         hk_scales = tile_at(16384 + 1024, [P, D], U8, "hk_scales")
         quantize(hk_codes[:], hk_scales[:], hk_dealt[:].rearrange("p j x -> p (j x)"))
         warm_bank = ps.tile([WARM_ROWS, I], F32, name="warm_bank")
+        product(warm_bank[:], hk_codes[:, :WARM_ROWS], hk_scales[:, :WARM_ROWS], hk_codes[:], hk_scales[:])
         key_words = tile_at(8192, [P, I], U32, "key_words")
-        for b in range(4):
+        for slots in (slice(0, P), slice(P, 2 * P), slice(2 * P, I)):
             nc.vector.tensor_copy(
-                key_words[:, b * P : (b + 1) * P],
-                pool_words[:].bitcast(U32).indirect(offsets[:, 8 * b : 8 * (b + 1)]),
+                key_words[:, slots],
+                pool_words[:].bitcast(U32).indirect(offsets[:, slots.start // 16 : slots.stop // 16]),
             )
 
         query_bf = tile([P, Q, PACK], BF16, "query_bf")
@@ -130,8 +131,6 @@ def tile_attend_rotatedscores_kernel(tc, query, hq, hk, keys_words, keys_scales,
                 )
             nc.scalar.copy(out=kr_bf[:, b * P : (b + 1) * P, :], in_=bank[:].rearrange("p j n -> p n j"))
 
-        product(warm_bank[:], hk_codes[:, :WARM_ROWS], hk_scales[:, :WARM_ROWS], key_words[:], key_scales[:])
-
         hq_codes = [tile([P, P], U32, "hq_codes%d" % j) for j in range(PACK)]
         hq_scales = [tile([P, P], U8, "hq_scales%d" % j) for j in range(PACK)]
         for half in range(2):
@@ -144,16 +143,19 @@ def tile_attend_rotatedscores_kernel(tc, query, hq, hk, keys_words, keys_scales,
             for j in range(PACK):
                 quantize(hq_codes[j][:, cols], hq_scales[j][:, cols], dealt[j])
 
-        qr_bank = ps.tile([P, PACK, Q], F32, name="qr_bank")
+        rows = [slice(0, Q // 2), slice(Q // 2, Q)]
+        qr_banks = [ps.tile([P, PACK, Q // 2], F32, name="qr_bank%d" % h, tag=tag) for h, tag in enumerate(("qr_bank", "kr_bank0"))]
         for j in range(PACK):
-            product(qr_bank[:, j, :], hq_codes[j][:], hq_scales[j][:], query_codes[:], query_scales[:])
+            for h in range(2):
+                product(qr_banks[h][:, j, :], hq_codes[j][:], hq_scales[j][:], query_codes[:, rows[h]], query_scales[:, rows[h]])
         product(warm_bank[:], hq_codes[3][:, :WARM_ROWS], hq_scales[3][:, :WARM_ROWS], key_words[:], key_scales[:])
         qr_bf = tile([P, Q, PACK], BF16, "qr_bf")
-        nc.scalar.copy(out=qr_bf[:], in_=qr_bank[:].rearrange("p j n -> p n j"))
+        nc.vector.tensor_copy(out=qr_bf[:, rows[0], :], in_=qr_banks[0][:].rearrange("p j n -> p n j"))
+        nc.scalar.copy(out=qr_bf[:, rows[1], :], in_=qr_banks[1][:].rearrange("p j n -> p n j"))
 
         kr_codes = tile_at(24576 + 2048 + 512 * 3, [P, I], U32, "kr_codes")
         kr_scales = tile([P, I], U8, "kr_scales")
-        for slots in (slice(0, I // 2), slice(I // 2, I)):
+        for slots in (slice(0, 3 * P), slice(3 * P, I)):
             quantize(kr_codes[:, slots], kr_scales[:, slots], kr_bf[:, slots, :].rearrange("p n j -> p (n j)"))
         qr_codes = tile([P, Q], U32, "qr_codes")
         qr_scales = tile([P, Q], U8, "qr_scales")

@@ -148,7 +148,7 @@ def tile_attend_rotatedscores_kernel(tc, query, hq, hk, keys_words, keys_scales,
         for j in range(PACK):
             for h in range(2):
                 product(qr_banks[h][:, j, :], hq_codes[j][:], hq_scales[j][:], query_codes[:, rows[h]], query_scales[:, rows[h]])
-        product(warm_bank[:], hq_codes[3][:, :WARM_ROWS], hq_scales[3][:, :WARM_ROWS], key_words[:], key_scales[:])
+        product(warm_bank[:], hq_codes[3][:, :WARM_ROWS], hq_scales[3][:, :WARM_ROWS], hk_codes[:], hk_scales[:])
         qr_bf = tile([P, Q, PACK], BF16, "qr_bf")
         nc.vector.tensor_copy(out=qr_bf[:, rows[0], :], in_=qr_banks[0][:].rearrange("p j n -> p n j"))
         nc.scalar.copy(out=qr_bf[:, rows[1], :], in_=qr_banks[1][:].rearrange("p j n -> p n j"))

@@ -118,45 +118,52 @@ def tile_attend_rotatedscores_kernel(tc, query, hq, hk, keys_words, keys_scales,
         query_scales = tile([P, Q], U8, "query_scales")
         quantize(query_codes[:], query_scales[:], query_bf[:].rearrange("p q t -> p (q t)"))
 
-        kr_bf = tile([P, I, PACK], BF16, "kr_bf", tag="query_raw")
-        for b in range(4):
-            bank = ps.tile([P, PACK, P], F32, name="kr_bank%d" % b)
+        def rotate_keys(block, copy, target):
+            bank = ps.tile([P, PACK, P], F32, name="kr_bank%d" % block)
             for j in range(PACK):
                 product(
                     bank[:, j, :],
                     hk_codes[:, j * P : (j + 1) * P],
                     hk_scales[:, j * P : (j + 1) * P],
-                    key_words[:, b * P : (b + 1) * P],
-                    key_scales[:, b * P : (b + 1) * P],
+                    key_words[:, block * P : (block + 1) * P],
+                    key_scales[:, block * P : (block + 1) * P],
                 )
-            nc.scalar.copy(out=kr_bf[:, b * P : (b + 1) * P, :], in_=bank[:].rearrange("p j n -> p n j"))
+            copy(out=target, in_=bank[:].rearrange("p j n -> p n j"))
+
+        kr_early = tile([P, 2 * P, PACK], BF16, "kr_early", tag="query_raw")
+        for block in range(2):
+            rotate_keys(block, nc.scalar.copy, kr_early[:, block * P : (block + 1) * P, :])
 
         hq_codes = [tile([P, P], U32, "hq_codes%d" % j) for j in range(PACK)]
         hq_scales = [tile([P, P], U8, "hq_scales%d" % j) for j in range(PACK)]
-        for half in range(2):
+        for half, groups in enumerate((((0, 2), (2, 3), (3, 4)), ((0, 1), (1, 2), (2, 3), (3, 4)))):
             dealt = []
-            for lo, hi in ((0, 2), (2, 3), (3, 4)):
+            for lo, hi in groups:
                 group = tile_at(24576 + 2048 * half + 512 * lo, [P, hi - lo, HALF], BF16, "hq_dealt%d%d" % (half, lo))
-                deal(nc.vector.tensor_copy, hq_raw[half][:], group[:], slice(lo, hi))
+                copy = nc.scalar.copy if (half, lo) == (1, 3) else nc.vector.tensor_copy
+                deal(copy, hq_raw[half][:], group[:], slice(lo, hi))
                 dealt += [group[:, j, :] for j in range(hi - lo)]
             cols = slice(half * (P // 2), (half + 1) * (P // 2))
             for j in range(PACK):
                 quantize(hq_codes[j][:, cols], hq_scales[j][:, cols], dealt[j])
 
-        rows = [slice(0, Q // 2), slice(Q // 2, Q)]
-        qr_banks = [ps.tile([P, PACK, Q // 2], F32, name="qr_bank%d" % h, tag=tag) for h, tag in enumerate(("qr_bank", "kr_bank0"))]
+        kr_third = tile_at(16384 + 1024 - 4096, [P, P, PACK], BF16, "kr_third")
+        rotate_keys(2, nc.scalar.copy, kr_third[:])
+        kr_codes = tile_at(24576 + 2048 + 512 * 2 - 2048 + 512, [P, I], U32, "kr_codes")
+        kr_scales = tile([P, I], U8, "kr_scales")
+        quantize(kr_codes[:, : 2 * P], kr_scales[:, : 2 * P], kr_early[:].rearrange("p n j -> p (n j)"))
+        kr_last = tile_at(24576 + 2048 + 512 * 3, [P, P, PACK], BF16, "kr_last")
+        rotate_keys(3, nc.vector.tensor_copy, kr_last[:])
+
+        qr_bank = ps.tile([P, PACK, Q], F32, name="qr_bank", tag="kr_bank0")
         for j in range(PACK):
-            for h in range(2):
-                product(qr_banks[h][:, j, :], hq_codes[j][:], hq_scales[j][:], query_codes[:, rows[h]], query_scales[:, rows[h]])
+            product(qr_bank[:, j, :], hq_codes[j][:], hq_scales[j][:], query_codes[:], query_scales[:])
         product(warm_bank[:], hq_codes[3][:, :WARM_ROWS], hq_scales[3][:, :WARM_ROWS], hk_codes[:], hk_scales[:])
         qr_bf = tile([P, Q, PACK], BF16, "qr_bf")
-        nc.vector.tensor_copy(out=qr_bf[:, rows[0], :], in_=qr_banks[0][:].rearrange("p j n -> p n j"))
-        nc.scalar.copy(out=qr_bf[:, rows[1], :], in_=qr_banks[1][:].rearrange("p j n -> p n j"))
-
-        kr_codes = tile_at(24576 + 2048 + 512 * 3, [P, I], U32, "kr_codes")
-        kr_scales = tile([P, I], U8, "kr_scales")
-        for slots in (slice(0, 3 * P), slice(3 * P, I)):
-            quantize(kr_codes[:, slots], kr_scales[:, slots], kr_bf[:, slots, :].rearrange("p n j -> p (n j)"))
+        nc.scalar.copy(out=qr_bf[:], in_=qr_bank[:].rearrange("p j n -> p n j"))
+        for block, values in ((2, kr_third), (3, kr_last)):
+            slots = slice(block * P, (block + 1) * P)
+            quantize(kr_codes[:, slots], kr_scales[:, slots], values[:].rearrange("p n j -> p (n j)"))
         qr_codes = tile([P, Q], U32, "qr_codes")
         qr_scales = tile([P, Q], U8, "qr_scales")
         quantize(qr_codes[:], qr_scales[:], qr_bf[:].rearrange("p q j -> p (q j)"))

@@ -144,29 +144,32 @@ def tile_attend_rotatedscores_kernel(tc, query, hq, hk, keys_words, keys_scales,
                 deal(copy, hq_raw[half][:], group[:], slice(lo, hi))
                 dealt += [group[:, j, :] for j in range(hi - lo)]
             cols = slice(half * (P // 2), (half + 1) * (P // 2))
-            for j in range(PACK):
+            for j in ((0, 1, 2, 3), (0, 1, 3, 2))[half]:
                 quantize(hq_codes[j][:, cols], hq_scales[j][:, cols], dealt[j])
 
         kr_third = tile_at(16384 + 1024 - 4096, [P, P, PACK], BF16, "kr_third")
         rotate_keys(2, nc.scalar.copy, kr_third[:])
-        kr_codes = tile_at(24576 + 2048 + 512 * 2 - 2048 + 512, [P, I], U32, "kr_codes")
+        kr_last = tile_at(24576 + 2048 - 512, [P, P, PACK], BF16, "kr_last")
+        rotate_keys(3, nc.vector.tensor_copy, kr_last[:])
+        kr_codes = tile_at(24576 + 2048 + 512 * 2, [P, I], U32, "kr_codes")
         kr_scales = tile([P, I], U8, "kr_scales")
         quantize(kr_codes[:, : 2 * P], kr_scales[:, : 2 * P], kr_early[:].rearrange("p n j -> p (n j)"))
-        kr_last = tile_at(24576 + 2048 + 512 * 3, [P, P, PACK], BF16, "kr_last")
-        rotate_keys(3, nc.vector.tensor_copy, kr_last[:])
 
         qr_bank = ps.tile([P, PACK, Q], F32, name="qr_bank", tag="kr_bank0")
-        for j in range(PACK):
+        for j in (0, 1, 3, 2):
             product(qr_bank[:, j, :], hq_codes[j][:], hq_scales[j][:], query_codes[:], query_scales[:])
-        product(warm_bank[:], hq_codes[3][:, :WARM_ROWS], hq_scales[3][:, :WARM_ROWS], hk_codes[:], hk_scales[:])
+        product(warm_bank[:], hq_codes[2][:, P // 2 : P // 2 + WARM_ROWS], hq_scales[2][:, P // 2 : P // 2 + WARM_ROWS], hk_codes[:], hk_scales[:])
         qr_bf = tile([P, Q, PACK], BF16, "qr_bf")
-        nc.scalar.copy(out=qr_bf[:], in_=qr_bank[:].rearrange("p j n -> p n j"))
+        rows = [slice(0, Q // 2), slice(Q // 2, Q)]
+        for part in rows:
+            nc.scalar.copy(out=qr_bf[:, part, :], in_=qr_bank[:, :, part].rearrange("p j n -> p n j"))
         for block, values in ((2, kr_third), (3, kr_last)):
             slots = slice(block * P, (block + 1) * P)
             quantize(kr_codes[:, slots], kr_scales[:, slots], values[:].rearrange("p n j -> p (n j)"))
         qr_codes = tile([P, Q], U32, "qr_codes")
         qr_scales = tile([P, Q], U8, "qr_scales")
-        quantize(qr_codes[:], qr_scales[:], qr_bf[:].rearrange("p q j -> p (q j)"))
+        for part in rows:
+            quantize(qr_codes[:, part], qr_scales[:, part], qr_bf[:, part, :].rearrange("p q j -> p (q j)"))
 
         scores = ps.tile([P, I], F32, name="scores")
         product(scores[:], qr_codes[:], qr_scales[:], kr_codes[:], kr_scales[:])

@@ -32,10 +32,10 @@ def tile_attend_rotatedscores_kernel(tc, query, hq, hk, keys_words, keys_scales,
         ps = ctx.enter_context(tc.psum_pool(name="ps", bufs=1))
 
         def tile(shape, dtype, name, tag=None):
-            return sb.tile(shape, dtype, name=name, tag=tag or name, align_bytes=64)
+            return sb.tile(shape, dtype, name=name, tag=tag or name, align_bytes=256)
 
         def tile_at(offset, shape, dtype, name):
-            return reused.tile(shape, dtype, name=name, align_bytes=64, offset=offset)
+            return reused.tile(shape, dtype, name=name, align_bytes=256, offset=offset)
 
         def deal(copy, raw, dealt, places):
             copy(
@@ -82,7 +82,7 @@ def tile_attend_rotatedscores_kernel(tc, query, hq, hk, keys_words, keys_scales,
                 in_=picked_scales[:].bitcast(I32)[SCALE_ROW0 + 4 * quad : SCALE_ROW0 + 4 * quad + 4, :],
             )
         hq_raw = [
-            tile_at(16384 + T - 128, [P, PACK, HALF], F32, "hq_raw0"),
+            tile_at(16384 + T - 256, [P, PACK, HALF], F32, "hq_raw0"),
             tile_at(16384 + 1024 - 4096, [P, PACK, HALF], F32, "hq_raw1"),
         ]
         for half in range(2):

@@ -180,8 +180,8 @@ def tile_attend_rotatedscores_kernel(tc, query, hq, hk, keys_words, keys_scales,
         nc.scalar.activation(weights[:], scores[:], ACT.Exp, bias=neg_max[:], accum_out=row_sum[:])
         inv_sum = tile([P, 1], F32, "inv_sum")
         nc.vector.reciprocal(inv_sum[:], row_sum[:])
-        for half, queue in enumerate((nc.scalar, nc.sync)):
+        for half in range(2):
             cols = slice(half * (I // 2), (half + 1) * (I // 2))
             result = tile([P, I // 2], F32, "result%d" % half)
             nc.vector.tensor_scalar(result[:], weights[:, cols], inv_sum[:], 512.0, ALU.mult, ALU.mult)
-            queue.dma_start(out=out[:, cols], in_=result[:])
+            nc.sync.dma_start(out=out[:, cols], in_=result[:])

@@ -39,8 +39,8 @@ def tile_attend_rotatedscores_kernel(tc, query, hq, hk, keys_words, keys_scales,
 
         def deal(copy, raw, dealt, places):
             copy(
-                out=dealt.rearrange("p j (u i t) -> p u j t i", i=4, t=PACK),
-                in_=raw.rearrange("p t (u j i) -> p u j t i", j=PACK, i=4)[:, :, places],
+                out=dealt.rearrange("p j (u i t) -> p u j t i", i=2, t=PACK),
+                in_=raw.rearrange("p t (u j i) -> p u j t i", j=PACK, i=2)[:, :, places],
             )
 
         def quantize(codes, scales, values):

@@ -128,7 +128,7 @@ def tile_attend_rotatedscores_kernel(tc, query, hq, hk, keys_words, keys_scales,
                     key_words[:, block * P : (block + 1) * P],
                     key_scales[:, block * P : (block + 1) * P],
                 )
-            copy(out=target, in_=bank[:].rearrange("p j n -> p n j"))
+            copy(out=target.rearrange("p (c i) j -> p c j i", i=2), in_=bank[:].rearrange("p j (c i) -> p c j i", i=2))
 
         kr_early = tile([P, 2 * P, PACK], BF16, "kr_early", tag="query_raw")
         for block in range(2):
@@ -162,7 +162,7 @@ def tile_attend_rotatedscores_kernel(tc, query, hq, hk, keys_words, keys_scales,
         qr_bf = tile([P, Q, PACK], BF16, "qr_bf")
         rows = [slice(0, Q // 2), slice(Q // 2, Q)]
         for part in rows:
-            nc.scalar.copy(out=qr_bf[:, part, :], in_=qr_bank[:, :, part].rearrange("p j n -> p n j"))
+            nc.scalar.copy(out=qr_bf[:, part, :].rearrange("p (c i) j -> p c j i", i=2), in_=qr_bank[:, :, part].rearrange("p j (c i) -> p c j i", i=2))
         for block, values in ((2, kr_third), (3, kr_last)):
             slots = slice(block * P, (block + 1) * P)
             quantize(kr_codes[:, slots], kr_scales[:, slots], values[:].rearrange("p n j -> p (n j)"))

@@ -78,8 +78,8 @@ def tile_attend_rotatedscores_kernel(tc, query, hq, hk, keys_words, keys_scales,
         nc.vector.memset(key_scales[:].bitcast(I32), 0)
         for quad in range(4):
             nc.sync.dma_start(
-                out=key_scales[:].bitcast(I32)[32 * quad : 32 * quad + 4, :],
-                in_=picked_scales[:].bitcast(I32)[SCALE_ROW0 + 4 * quad : SCALE_ROW0 + 4 * quad + 4, :],
+                out=key_scales[:].bitcast(I32)[quad:P:32, :],
+                in_=picked_scales[:].bitcast(I32)[SCALE_ROW0 + quad : P : 4, :],
             )
         hq_raw = [
             tile_at(16384 + T - 256, [P, PACK, HALF], F32, "hq_raw0"),

from contextlib import ExitStack

import concourse.mybir as mybir

K, D, T, I, Q = 512, 512, 2048, 512, 128
FLOPS = 2 * K * D * Q + 2 * K * D * I + 2 * D * Q * I

F32 = mybir.dt.float32
BF16 = mybir.dt.bfloat16
I32 = mybir.dt.int32
U32 = mybir.dt.uint32
U16 = mybir.dt.uint16
U8 = mybir.dt.uint8
FP8X4 = mybir.dt.float8_e4m3fn_x4
ALU = mybir.AluOpType
ACT = mybir.ActivationFunctionType
AX = mybir.AxisListType

P = 128
PACK = 4
HALF = D // 2
HK_SCALAR_COLS = 192
SCALE_ROW0 = P - 16
WARM_ROWS = 32


def tile_attend_rotatedscores_kernel(tc, query, hq, hk, keys_words, keys_scales, offs, out):
    nc = tc.nc
    with ExitStack() as ctx:
        sb = ctx.enter_context(tc.tile_pool(name="sb", bufs=1))
        reused = ctx.enter_context(tc.tile_pool(name="reused", bufs=1))
        ps = ctx.enter_context(tc.psum_pool(name="ps", bufs=1))

        def tile(shape, dtype, name, tag=None):
            return sb.tile(shape, dtype, name=name, tag=tag or name, align_bytes=256)

        def tile_at(offset, shape, dtype, name):
            return reused.tile(shape, dtype, name=name, align_bytes=256, offset=offset)

        def deal(copy, raw, dealt, places):
            copy(
                out=dealt.rearrange("p j (u i t) -> p u j t i", i=2, t=PACK),
                in_=raw.rearrange("p t (u j i) -> p u j t i", j=PACK, i=2)[:, :, places],
            )

        def quantize(codes, scales, values):
            nc.vector.quantize_mx(out=codes.bitcast(FP8X4), scales=scales, in_=values)

        def product(bank, lhs_codes, lhs_scales, rhs_codes, rhs_scales):
            nc.tensor.matmul_mx(
                out=bank,
                lhsT=lhs_codes.bitcast(FP8X4),
                lhsT_scale=lhs_scales,
                rhs=rhs_codes.bitcast(FP8X4),
                rhs_scale=rhs_scales,
                start=True,
                stop=True,
            )

        offsets = sb.tile([P, I // 16], U16, name="offsets")
        pool_scales = tile_at(16384, [P, T], U8, "pool_scales")
        pool_words = tile_at(0, [P, T], I32, "pool_words")
        hk_raw = tile([P, PACK, D], F32, "hk_raw")
        query_raw = tile([P, PACK, Q], F32, "query_raw")
        hk_rows = hk.rearrange("(p t) d -> p t d", t=PACK)
        hq_rows = hq.rearrange("(p t) d -> p t d", t=PACK)

        nc.vector.memset(pool_scales[:].bitcast(I32)[:SCALE_ROW0, :], 0)
        nc.sync.dma_start(offsets[:], offs)
        nc.scalar.dma_start(out=pool_scales[:].bitcast(I32)[SCALE_ROW0:, :], in_=keys_scales[0].bitcast(I32))
        nc.scalar.dma_start(out=hk_raw[:, 0:2, :], in_=hk_rows[:, 0:2, :])
        nc.sync.dma_start(out=hk_raw[:, 2:4, :], in_=hk_rows[:, 2:4, :])
        nc.sync.dma_start(out=pool_words[:], in_=keys_words[0].rearrange("p n t -> p (n t)").bitcast(I32))
        nc.sync.dma_start(out=query_raw[:], in_=query.rearrange("(p t) q -> p t q", t=PACK))
        picked_scales = tile([P, I], U8, "picked_scales")
        nc.vector.tensor_copy(picked_scales[:], pool_scales[:].indirect(offsets[:]))
        key_scales = tile([P, I], U8, "key_scales")
        nc.vector.memset(key_scales[:].bitcast(I32), 0)
        for quad in range(4):
            nc.sync.dma_start(
                out=key_scales[:].bitcast(I32)[quad:P:32, :],
                in_=picked_scales[:].bitcast(I32)[SCALE_ROW0 + quad : P : 4, :],
            )
        hq_raw = [
            tile_at(16384 + T - 256, [P, PACK, HALF], F32, "hq_raw0"),
            tile_at(16384 + 1024 - 4096, [P, PACK, HALF], F32, "hq_raw1"),
        ]
        for half in range(2):
            nc.sync.dma_start(out=hq_raw[half][:], in_=hq_rows[:, :, half * HALF : (half + 1) * HALF])

        warm_in = tile([P, 8], F32, "warm_in")
        warm_out = tile([P, 8], F32, "warm_out")
        nc.vector.memset(warm_in[:], 0.0)
        nc.scalar.activation(warm_out[:], warm_in[:], ACT.Exp)

        hk_dealt = tile_at(8192, [P, PACK, D], BF16, "hk_dealt")
        every = slice(0, PACK)
        deal(nc.scalar.copy, hk_raw[:, :, :HK_SCALAR_COLS], hk_dealt[:, :, :HK_SCALAR_COLS], every)
        deal(nc.vector.tensor_copy, hk_raw[:, :, HK_SCALAR_COLS:], hk_dealt[:, :, HK_SCALAR_COLS:], every)
        hk_codes = tile([P, D], U32, "hk_codes")
        hk_scales = tile_at(16384 + 1024, [P, D], U8, "hk_scales")
        quantize(hk_codes[:], hk_scales[:], hk_dealt[:].rearrange("p j x -> p (j x)"))
        warm_bank = ps.tile([WARM_ROWS, I], F32, name="warm_bank")
        product(warm_bank[:], hk_codes[:, :WARM_ROWS], hk_scales[:, :WARM_ROWS], hk_codes[:], hk_scales[:])
        key_words = tile_at(8192, [P, I], U32, "key_words")
        for slots in (slice(0, P), slice(P, 2 * P), slice(2 * P, I)):
            nc.vector.tensor_copy(
                key_words[:, slots],
                pool_words[:].bitcast(U32).indirect(offsets[:, slots.start // 16 : slots.stop // 16]),
            )

        query_bf = tile([P, Q, PACK], BF16, "query_bf")
        nc.scalar.copy(
            out=query_bf[:].rearrange("p (c i) t -> p c t i", i=4),
            in_=query_raw[:].rearrange("p t (c i) -> p c t i", i=4),
        )
        query_codes = tile([P, Q], U32, "query_codes")
        query_scales = tile([P, Q], U8, "query_scales")
        quantize(query_codes[:], query_scales[:], query_bf[:].rearrange("p q t -> p (q t)"))

        def rotate_keys(block, copy, target):
            bank = ps.tile([P, PACK, P], F32, name="kr_bank%d" % block)
            for j in range(PACK):
                product(
                    bank[:, j, :],
                    hk_codes[:, j * P : (j + 1) * P],
                    hk_scales[:, j * P : (j + 1) * P],
                    key_words[:, block * P : (block + 1) * P],
                    key_scales[:, block * P : (block + 1) * P],
                )
            copy(out=target.rearrange("p (c i) j -> p c j i", i=2), in_=bank[:].rearrange("p j (c i) -> p c j i", i=2))

        kr_early = tile([P, 2 * P, PACK], BF16, "kr_early", tag="query_raw")
        for block in range(2):
            rotate_keys(block, nc.scalar.copy, kr_early[:, block * P : (block + 1) * P, :])

        hq_codes = [tile([P, P], U32, "hq_codes%d" % j) for j in range(PACK)]
        hq_scales = [tile([P, P], U8, "hq_scales%d" % j) for j in range(PACK)]
        for half, groups in enumerate((((0, 2), (2, 3), (3, 4)), ((0, 1), (1, 2), (2, 3), (3, 4)))):
            dealt = []
            for lo, hi in groups:
                group = tile_at(24576 + 2048 * half + 512 * lo, [P, hi - lo, HALF], BF16, "hq_dealt%d%d" % (half, lo))
                copy = nc.scalar.copy if (half, lo) == (1, 3) else nc.vector.tensor_copy
                deal(copy, hq_raw[half][:], group[:], slice(lo, hi))
                dealt += [group[:, j, :] for j in range(hi - lo)]
            cols = slice(half * (P // 2), (half + 1) * (P // 2))
            for j in ((0, 1, 2, 3), (0, 1, 3, 2))[half]:
                quantize(hq_codes[j][:, cols], hq_scales[j][:, cols], dealt[j])

        kr_third = tile_at(16384 + 1024 - 4096, [P, P, PACK], BF16, "kr_third")
        rotate_keys(2, nc.scalar.copy, kr_third[:])
        kr_last = tile_at(24576 + 2048 - 512, [P, P, PACK], BF16, "kr_last")
        rotate_keys(3, nc.vector.tensor_copy, kr_last[:])
        kr_codes = tile_at(24576 + 2048 + 512 * 2, [P, I], U32, "kr_codes")
        kr_scales = tile([P, I], U8, "kr_scales")
        quantize(kr_codes[:, : 2 * P], kr_scales[:, : 2 * P], kr_early[:].rearrange("p n j -> p (n j)"))

        qr_bank = ps.tile([P, PACK, Q], F32, name="qr_bank", tag="kr_bank0")
        for j in (0, 1, 3, 2):
            product(qr_bank[:, j, :], hq_codes[j][:], hq_scales[j][:], query_codes[:], query_scales[:])
        product(warm_bank[:], hq_codes[2][:, P // 2 : P // 2 + WARM_ROWS], hq_scales[2][:, P // 2 : P // 2 + WARM_ROWS], hk_codes[:], hk_scales[:])
        qr_bf = tile([P, Q, PACK], BF16, "qr_bf")
        rows = [slice(0, Q // 2), slice(Q // 2, Q)]
        for part in rows:
            nc.scalar.copy(out=qr_bf[:, part, :].rearrange("p (c i) j -> p c j i", i=2), in_=qr_bank[:, :, part].rearrange("p j (c i) -> p c j i", i=2))
        for block, values in ((2, kr_third), (3, kr_last)):
            slots = slice(block * P, (block + 1) * P)
            quantize(kr_codes[:, slots], kr_scales[:, slots], values[:].rearrange("p n j -> p (n j)"))
        qr_codes = tile([P, Q], U32, "qr_codes")
        qr_scales = tile([P, Q], U8, "qr_scales")
        for part in rows:
            quantize(qr_codes[:, part], qr_scales[:, part], qr_bf[:, part, :].rearrange("p q j -> p (q j)"))

        scores = ps.tile([P, I], F32, name="scores")
        product(scores[:], qr_codes[:], qr_scales[:], kr_codes[:], kr_scales[:])
        neg_max = tile([P, 1], F32, "neg_max")
        nc.vector.tensor_reduce(neg_max[:], scores[:], AX.X, ALU.max, negate=True)
        weights = tile([P, I], F32, "weights")
        row_sum = tile([P, 1], F32, "row_sum")
        nc.scalar.activation(weights[:], scores[:], ACT.Exp, bias=neg_max[:], accum_out=row_sum[:])
        inv_sum = tile([P, 1], F32, "inv_sum")
        nc.vector.reciprocal(inv_sum[:], row_sum[:])
        for half in range(2):
            cols = slice(half * (I // 2), (half + 1) * (I // 2))
            result = tile([P, I // 2], F32, "result%d" % half)
            nc.vector.tensor_scalar(result[:], weights[:, cols], inv_sum[:], 512.0, ALU.mult, ALU.mult)
            nc.sync.dma_start(out=out[:, cols], in_=result[:])
